import numpy as np
import ml_dtypes


def mxq(x, axis, fmt="e4m3"):
    dtype, down = {"e4m3": (ml_dtypes.float8_e4m3fn, 7), "e5m2": (ml_dtypes.float8_e5m2, 14)}[fmt]
    v = np.moveaxis(np.asarray(x, np.float32).astype(ml_dtypes.bfloat16).astype(np.float64), axis, -1)
    blocks = v.reshape(v.shape[:-1] + (-1, 32))
    amax = np.abs(blocks).max(-1, keepdims=True)
    byte = np.maximum(np.where(amax > 0, np.frexp(amax)[1] - 1 + 127, 0) - down, 1)
    scale = np.exp2(byte - 127.0)
    codes = (blocks / scale).astype(np.float32).astype(dtype).astype(np.float64)
    return np.moveaxis((codes * scale).reshape(v.shape), -1, axis)


WIDE = False


def mx_kscale(k):
    if not WIDE:
        return np.ones(k)
    levels = np.array([10, -10, 5, -5, 0])
    if k % 512:
        return np.exp2(np.random.permutation(np.resize(levels, k // 32))).repeat(32)
    a = np.empty((k // 512, 16))
    for p in range(k // 512):
        a[p, :8] = np.random.permutation(np.resize(levels, 8))
        for g in range(8):
            far = levels[np.abs(levels - a[p, g]) >= 10]
            a[p, g + 8] = far[np.random.randint(len(far))]
    return np.exp2(a.ravel()).repeat(32)


def f64(x):
    return np.asarray(x).astype(np.float64)


def striped(idx):
    return np.tile(idx.reshape(-1, 16).T, (8, 1)).astype(np.uint16)


def unstriped(offs):
    return offs[:16].T.reshape(-1).astype(np.int64)


def striped8(idx):
    return np.concatenate([v.reshape(-1, 16).T for v in idx]).astype(np.uint16)


def unstriped8(offs):
    return np.stack([offs[16 * g:16 * g + 16].T.reshape(-1) for g in range(8)]).astype(np.int64)


E2M1 = np.array([0.0, 0.5, 1.0, 1.5, 2.0, 3.0, 4.0, 6.0, -0.0, -0.5, -1.0, -1.5, -2.0, -3.0, -4.0, -6.0])


def pack_weight(w, fmt):
    k, n = w.shape
    w = f64(np.asarray(w, np.float32).astype(ml_dtypes.bfloat16)).reshape(k // 32, 32, n)
    amax = np.abs(w).max(1)
    if fmt == "e4m3":
        byte = np.frexp(amax)[1] - 1 + 127 - 7
    else:
        mant, ex = np.frexp(amax / 6.0)
        byte = np.where(mant > 0.5, ex, ex - 1) + 127
    byte = np.clip(np.where(amax > 0, byte, 1), 1, 254)
    scaled = (w * np.exp2(127.0 - byte)[:, None, :]).reshape(k, n).astype(np.float32)
    by_word = np.ascontiguousarray(scaled.reshape(k // 512, 128, 4, n).transpose(0, 1, 3, 2))
    if fmt == "e4m3":
        words = by_word.astype(ml_dtypes.float8_e4m3fn).view(np.uint8)
    else:
        c = by_word.astype(ml_dtypes.float4_e2m1fn).view(np.uint8) & 0xF
        words = (c[..., 0::2] | (c[..., 1::2] << 4)).reshape(k // 512, 128, 2 * n)
    return np.ascontiguousarray(words), np.ascontiguousarray(byte.astype(np.uint8).reshape(k // 512, 16, n))


def unpack_weight(words, scales, fmt):
    g, _, n = scales.shape
    words = np.ascontiguousarray(words).reshape(g, 128, n, -1)
    if fmt == "e4m3":
        vals = words.view(ml_dtypes.float8_e4m3fn).astype(np.float64)
    else:
        nib = np.empty((g, 128, n, 4), np.uint8)
        nib[..., 0::2] = words & 0xF
        nib[..., 1::2] = words >> 4
        vals = E2M1[nib]
    vals = vals * np.repeat(np.exp2(scales.astype(np.float64) - 127.0), 8, axis=1)[..., None]
    return vals.transpose(0, 1, 3, 2).reshape(g * 512, n)


def pack_table(v):
    words, scales = pack_weight(v, "e4m3")
    return np.concatenate([words.reshape(words.shape[0], -1), scales.reshape(scales.shape[0], -1)], axis=1)


def unpack_table(tab):
    g, t = tab.shape[0], tab.shape[1] // 528
    return unpack_weight(tab[:, :512 * t].reshape(g, 128, t, 4), tab[:, 512 * t:].reshape(g, 16, t), "e4m3")


K, M, T, S = 1536, 512, 512, 256


def setup_inputs():
    n = np.random.standard_normal
    s = mx_kscale(K)[:, None]
    s2 = mx_kscale(512)[:, None]
    p_w4 = pack_weight(n((K, M)) / np.sqrt(K) / s, "e2m1")
    return {
        "tab": pack_table(n((K, T)) * s),
        "w4_words": p_w4[0],
        "w4_scales": p_w4[1],
        "c": (n((512, S)) * s2).astype(np.float32),
        "u": (n((512, M)) / np.sqrt(512) / s2).astype(np.float32),
        "b": (0.3 * n(512)).astype(np.float32),
        "wgo": np.repeat(np.random.uniform(0.5, 2.0, (8, S)), 16, axis=0).astype(np.float32),
        "offs": striped(np.random.permutation(T)[:S]),
        "offs2": striped8(np.stack([np.random.permutation(T)[:S] for _ in range(8)])),
    }


def reference(tab, w4_words, w4_scales, c, u, b, wgo, offs, offs2):
    tab_ = unpack_table(tab)[:, unstriped(offs)]
    w4_ = unpack_weight(w4_words, w4_scales, "e2m1")
    c_ = mxq(f64(c), 0, "e4m3")
    u_ = mxq(f64(u), 0, "e4m3")
    y = w4_.T @ tab_ + u_.T @ c_
    place = unstriped8(offs2)[np.arange(M) % 128 // 16]
    out = np.zeros((M, T))
    out[np.arange(M)[:, None], place] = f64(wgo)[np.arange(M) % 128] * (y + f64(b)[:, None])
    return out

@@ -1,0 +1,184 @@
+from contextlib import ExitStack
+
+import concourse.mybir as mybir
+from concourse.masks import make_identity
+
+K, M, T, S = 1536, 512, 512, 256
+L = 512
+FLOPS = 2 * (K + L) * M * S
+
+F32 = mybir.dt.float32
+BF16 = mybir.dt.bfloat16
+I32 = mybir.dt.int32
+U32 = mybir.dt.uint32
+U16 = mybir.dt.uint16
+U8 = mybir.dt.uint8
+FP8X4 = mybir.dt.float8_e4m3fn_x4
+FP4X4 = mybir.dt.float4_e2m1fn_x4
+IDENTITY = mybir.ActivationFunctionType.Identity
+COPY = mybir.ActivationFunctionType.Copy
+MULT = mybir.AluOpType.mult
+
+P = 128
+PACK = 4
+PASSES = K // (P * PACK)
+ROW_TILES = M // P
+HALF = 128
+HALVES = S // HALF
+
+
+def tile_list_tabhs_d_bias_kernel(tc, tab, w4_words, w4_scales, c, u, b, wgo, offs, offs2, out):
+    nc = tc.nc
+    with ExitStack() as ctx:
+        keep = ctx.enter_context(tc.tile_pool(name="keep", bufs=1))
+        psum = ctx.enter_context(tc.psum_pool(name="psum", bufs=1))
+
+        pick = keep.tile([P, S // 16], U16, name="pick")
+        place = keep.tile([P, S // 16], U16, name="place")
+        tab_planes = keep.tile([P, PASSES, T // 4], I32, name="tab_planes", align_bytes=64)
+        w_planes = keep.tile([P, PASSES, M // 4], I32, name="w_planes", align_bytes=64)
+        tab_words = [keep.tile([P, T], I32, name="tab_words%d" % a, align_bytes=64) for a in range(PASSES)]
+        w_words = keep.tile([P, PASSES, 2 * M], U8, name="w_words", align_bytes=64)
+        c_raw = keep.tile([P, PACK, S], F32, name="c_raw")
+        u_raw0 = keep.tile([P, PACK, P], F32, name="u_raw0")
+        u_raw1 = keep.tile([P, PACK, P], F32, name="u_raw1")
+        u_raw23 = keep.tile([P, PACK, 2 * P], F32, name="u_raw23")
+        weights = keep.tile([P, S], F32, name="weights")
+        b_rows = keep.tile([P, P], F32, name="b_rows")
+        ident = keep.tile([P, P], F32, name="ident")
+        bias = keep.tile([P, ROW_TILES], F32, name="bias")
+        placed = [keep.tile([P, T], F32, name="placed%d" % m) for m in range(ROW_TILES)]
+
+        tab32 = tab.bitcast(I32)
+        w_scales32 = w4_scales.bitcast(I32)
+        u_rows = u.rearrange("(p j) n -> p j n", j=PACK)
+
+        nc.vector.memset(tab_planes[:], 0)
+        nc.vector.memset(w_planes[:], 0)
+        nc.sync.dma_start(pick[:], offs)
+        nc.sync.dma_start(c_raw[:], c.rearrange("(p j) s -> p j s", j=PACK))
+        first = P * T
+        for q in range(4):
+            rows = tab32[:, first + q * T : first + (q + 1) * T].rearrange("a (r t) -> r a t", r=4)
+            nc.scalar.dma_start(tab_planes[32 * q : 32 * q + 4, :, :], rows)
+        nc.sync.dma_start(u_raw0[:], u_rows[:, :, 0:P])
+        for a in range(PASSES):
+            nc.sync.dma_start(tab_words[a][:], tab32[a, 0:first].rearrange("(p t) -> p t", p=P))
+        nc.sync.dma_start(place[:], offs2)
+        for q in range(4):
+            rows = w_scales32[:, 4 * q : 4 * q + 4, :].rearrange("a r n -> r a n")
+            nc.sync.dma_start(w_planes[32 * q : 32 * q + 4, :, :], rows)
+        nc.sync.dma_start(w_words[:].bitcast(I32), w4_words.bitcast(I32).rearrange("a p n -> p a n"))
+        nc.sync.dma_start(u_raw1[:], u_rows[:, :, P : 2 * P])
+        nc.sync.dma_start(u_raw23[:], u_rows[:, :, 2 * P : 4 * P])
+
+        nc.gpsimd.memset(b_rows[:], 0.0)
+        nc.gpsimd.dma_start(b_rows[0:ROW_TILES, :], b.rearrange("(m p) -> m p", p=P))
+        nc.gpsimd.dma_start(weights[:], wgo)
+        make_identity(nc, ident[:])
+        for m in range(ROW_TILES):
+            nc.vector.memset(placed[m][:], 0.0)
+
+        def interleave(raw, width, name):
+            grouped = keep.tile([P, width, PACK], BF16, name=name, align_bytes=64)
+            nc.scalar.activation(
+                grouped[:].rearrange("p (w i) j -> p w j i", i=4),
+                raw.rearrange("p j (w i) -> p w j i", i=4),
+                COPY,
+            )
+            return grouped
+
+        def quantize(grouped, width, name):
+            codes = keep.tile([P, width], U32, name=name + "_codes", align_bytes=64)
+            scales = keep.tile([P, width], U8, name=name + "_scales", align_bytes=64)
+            nc.vector.quantize_mx(
+                out=codes[:].bitcast(FP8X4),
+                scales=scales[:],
+                in_=grouped[:].rearrange("p w j -> p (w j)"),
+            )
+            return codes, scales
+
+        c_bf = interleave(c_raw[:], S, "c_bf")
+        u_bf = [interleave(u_raw0[:], P, "u_bf0")]
+
+        b_t = psum.tile([P, P], F32, name="b_t", tag="bank7")
+        nc.tensor.transpose(b_t[:], b_rows[:], ident[:])
+        nc.scalar.activation(bias[:], b_t[:, 0:ROW_TILES], COPY)
+
+        got_scales = []
+        for a in range(PASSES):
+            got = keep.tile([P, S], U8, name="got_scales%d" % a, align_bytes=64)
+            nc.vector.tensor_copy(got[:], tab_planes[:, a, :].bitcast(U8).indirect(pick[:]))
+            got_scales.append(got)
+        got_words = []
+
+        def gather_words(a):
+            got = keep.tile([P, S], U32, name="got_words%d" % a, align_bytes=64)
+            nc.vector.tensor_copy(got[:], tab_words[a][:].bitcast(U32).indirect(pick[:]))
+            got_words.append(got)
+
+        gather_words(0)
+        c_codes, c_scales = quantize(c_bf, S, "c")
+        gather_words(1)
+        u_q = [quantize(u_bf[0], P, "u0")]
+        gather_words(2)
+
+        def product(m, h):
+            acc = psum.tile([P, HALF], F32, name="acc%d" % (2 * m + h), tag="bank%d" % (2 * m + h))
+            cols = slice(h * HALF, (h + 1) * HALF)
+            nc.tensor.matmul_mx(
+                out=acc[:],
+                lhsT=u_q[m][0][:].bitcast(FP8X4),
+                lhsT_scale=u_q[m][1][:],
+                rhs=c_codes[:, cols].bitcast(FP8X4),
+                rhs_scale=c_scales[:, cols],
+                start=True,
+                stop=False,
+            )
+            for a in range(PASSES):
+                nc.tensor.matmul_mx(
+                    out=acc[:],
+                    lhsT=w_words[:, a, 2 * P * m : 2 * P * (m + 1)].bitcast(FP4X4),
+                    lhsT_scale=w_planes[:, a, :].bitcast(U8)[:, P * m : P * (m + 1)],
+                    rhs=got_words[a][:, cols].bitcast(FP8X4),
+                    rhs_scale=got_scales[a][:, cols],
+                    start=False,
+                    stop=(a == PASSES - 1),
+                )
+            y = keep.tile([P, HALF], F32, name="y%d" % (2 * m + h))
+            nc.scalar.activation(y[:], acc[:], IDENTITY, bias=bias[:, m : m + 1])
+            return y
+
+        def scatter(m, h, y):
+            offsets = place[:, h * HALF // 16 : (h + 1) * HALF // 16]
+            nc.vector.tensor_tensor(placed[m][:].indirect(offsets), y[:], weights[:, h * HALF : (h + 1) * HALF], MULT)
+
+        def store(m):
+            nc.sync.dma_start(out[m * P : (m + 1) * P, :], placed[m][:])
+
+        y00 = product(0, 0)
+        y01 = product(0, 1)
+        u_bf.append(interleave(u_raw1[:], P, "u_bf1"))
+        scatter(0, 0, y00)
+        u_q.append(quantize(u_bf[1], P, "u1"))
+        scatter(0, 1, y01)
+        store(0)
+        y10 = product(1, 0)
+        y11 = product(1, 1)
+        u_bf.append(interleave(u_raw23[:, :, 0:P], P, "u_bf2"))
+        u_bf.append(interleave(u_raw23[:, :, P : 2 * P], P, "u_bf3"))
+        scatter(1, 0, y10)
+        u_q.append(quantize(u_bf[2], P, "u2"))
+        scatter(1, 1, y11)
+        store(1)
+        u_q.append(quantize(u_bf[3], P, "u3"))
+        y20 = product(2, 0)
+        y30 = product(3, 0)
+        y21 = product(2, 1)
+        y31 = product(3, 1)
+        scatter(2, 0, y20)
+        scatter(3, 0, y30)
+        scatter(2, 1, y21)
+        store(2)
+        scatter(3, 1, y31)
+        store(3)

@@ -54,28 +54,28 @@ def tile_list_tabhs_d_bias_kernel(tc, tab, w4_words, w4_scales, c, u, b, wgo, of
         u_rows = u.rearrange("(p j) n -> p j n", j=PACK)
 
         nc.vector.memset(tab_planes[:], 0)
-        nc.vector.memset(w_planes[:], 0)
         nc.sync.dma_start(pick[:], offs)
-        nc.sync.dma_start(c_raw[:], c.rearrange("(p j) s -> p j s", j=PACK))
+        nc.sync.dma_start(tab_words[0][:], tab32[0, 0 : P * T].rearrange("(p t) -> p t", p=P))
+        nc.sync.dma_start(tab_words[1][:], tab32[1, 0 : P * T].rearrange("(p t) -> p t", p=P))
         first = P * T
         for q in range(4):
             rows = tab32[:, first + q * T : first + (q + 1) * T].rearrange("a (r t) -> r a t", r=4)
-            nc.scalar.dma_start(tab_planes[32 * q : 32 * q + 4, :, :], rows)
+            nc.sync.dma_start(tab_planes[32 * q : 32 * q + 4, :, :], rows)
+        nc.sync.dma_start(c_raw[:], c.rearrange("(p j) s -> p j s", j=PACK))
         nc.sync.dma_start(u_raw0[:], u_rows[:, :, 0:P])
-        for a in range(PASSES):
-            nc.sync.dma_start(tab_words[a][:], tab32[a, 0:first].rearrange("(p t) -> p t", p=P))
-        nc.sync.dma_start(place[:], offs2)
+        nc.sync.dma_start(tab_words[2][:], tab32[2, 0 : P * T].rearrange("(p t) -> p t", p=P))
+        nc.sync.dma_start(w_words[:].bitcast(I32), w4_words.bitcast(I32).rearrange("a p n -> p a n"))
+        nc.vector.memset(w_planes[:], 0)
         for q in range(4):
             rows = w_scales32[:, 4 * q : 4 * q + 4, :].rearrange("a r n -> r a n")
             nc.sync.dma_start(w_planes[32 * q : 32 * q + 4, :, :], rows)
-        nc.sync.dma_start(w_words[:].bitcast(I32), w4_words.bitcast(I32).rearrange("a p n -> p a n"))
         nc.sync.dma_start(u_raw1[:], u_rows[:, :, P : 2 * P])
+        nc.sync.dma_start(place[:], offs2)
         nc.sync.dma_start(u_raw23[:], u_rows[:, :, 2 * P : 4 * P])
-
+        make_identity(nc, ident[:])
         nc.gpsimd.memset(b_rows[:], 0.0)
         nc.gpsimd.dma_start(b_rows[0:ROW_TILES, :], b.rearrange("(m p) -> m p", p=P))
         nc.gpsimd.dma_start(weights[:], wgo)
-        make_identity(nc, ident[:])
         for m in range(ROW_TILES):
             nc.vector.memset(placed[m][:], 0.0)
 
@@ -98,30 +98,34 @@ def tile_list_tabhs_d_bias_kernel(tc, tab, w4_words, w4_scales, c, u, b, wgo, of
             )
             return codes, scales
 
-        c_bf = interleave(c_raw[:], S, "c_bf")
+        c_bf = [interleave(c_raw[:, :, 0:HALF], HALF, "c_bf0")]
         u_bf = [interleave(u_raw0[:], P, "u_bf0")]
+        c_bf.append(interleave(c_raw[:, :, HALF:S], HALF, "c_bf1"))
 
         b_t = psum.tile([P, P], F32, name="b_t", tag="bank7")
         nc.tensor.transpose(b_t[:], b_rows[:], ident[:])
         nc.scalar.activation(bias[:], b_t[:, 0:ROW_TILES], COPY)
 
-        got_scales = []
+        got_scales = [keep.tile([P, S], U8, name="got_scales%d" % a, align_bytes=64) for a in range(PASSES)]
+        got_words = [keep.tile([P, S], U32, name="got_words%d" % a, align_bytes=64) for a in range(PASSES)]
+
+        def gather_scales(a, lo, hi):
+            window = tab_planes[:, a, :].bitcast(U8)
+            nc.vector.tensor_copy(got_scales[a][:, lo:hi], window.indirect(pick[:, lo // 16 : hi // 16]))
+
+        def gather_words(a, lo, hi):
+            window = tab_words[a][:].bitcast(U32)
+            nc.vector.tensor_copy(got_words[a][:, lo:hi], window.indirect(pick[:, lo // 16 : hi // 16]))
+
+        gather_words(0, 0, S)
+        gather_words(1, 0, S)
         for a in range(PASSES):
-            got = keep.tile([P, S], U8, name="got_scales%d" % a, align_bytes=64)
-            nc.vector.tensor_copy(got[:], tab_planes[:, a, :].bitcast(U8).indirect(pick[:]))
-            got_scales.append(got)
-        got_words = []
-
-        def gather_words(a):
-            got = keep.tile([P, S], U32, name="got_words%d" % a, align_bytes=64)
-            nc.vector.tensor_copy(got[:], tab_words[a][:].bitcast(U32).indirect(pick[:]))
-            got_words.append(got)
-
-        gather_words(0)
-        c_codes, c_scales = quantize(c_bf, S, "c")
-        gather_words(1)
+            gather_scales(a, 0, S)
+        c_q = [quantize(c_bf[0], HALF, "c0")]
+        gather_words(2, 0, HALF)
         u_q = [quantize(u_bf[0], P, "u0")]
-        gather_words(2)
+        gather_words(2, HALF, S)
+        c_q.append(quantize(c_bf[1], HALF, "c1"))
 
         def product(m, h):
             acc = psum.tile([P, HALF], F32, name="acc%d" % (2 * m + h), tag="bank%d" % (2 * m + h))
@@ -130,8 +134,8 @@ def tile_list_tabhs_d_bias_kernel(tc, tab, w4_words, w4_scales, c, u, b, wgo, of
                 out=acc[:],
                 lhsT=u_q[m][0][:].bitcast(FP8X4),
                 lhsT_scale=u_q[m][1][:],
-                rhs=c_codes[:, cols].bitcast(FP8X4),
-                rhs_scale=c_scales[:, cols],
+                rhs=c_q[h][0][:].bitcast(FP8X4),
+                rhs_scale=c_q[h][1][:],
                 start=True,
                 stop=False,
             )

@@ -1,7 +1,6 @@
 from contextlib import ExitStack
 
 import concourse.mybir as mybir
-from concourse.masks import make_identity
 
 K, M, T, S = 1536, 512, 512, 256
 L = 512
@@ -38,14 +37,11 @@ def tile_list_tabhs_d_bias_kernel(tc, tab, w4_words, w4_scales, c, u, b, wgo, of
         tab_planes = keep.tile([P, PASSES, T // 4], I32, name="tab_planes", align_bytes=64)
         w_planes = keep.tile([P, PASSES, M // 4], I32, name="w_planes", align_bytes=64)
         tab_words = [keep.tile([P, T], I32, name="tab_words%d" % a, align_bytes=64) for a in range(PASSES)]
-        w_words = keep.tile([P, PASSES, 2 * M], U8, name="w_words", align_bytes=64)
+        w_words = [keep.tile([P, PASSES, M], U8, name="w_words%d" % i, align_bytes=64) for i in range(2)]
         c_raw = keep.tile([P, PACK, S], F32, name="c_raw")
-        u_raw0 = keep.tile([P, PACK, P], F32, name="u_raw0")
-        u_raw1 = keep.tile([P, PACK, P], F32, name="u_raw1")
+        u_raw01 = keep.tile([P, PACK, 2 * P], F32, name="u_raw01")
         u_raw23 = keep.tile([P, PACK, 2 * P], F32, name="u_raw23")
         weights = keep.tile([P, S], F32, name="weights")
-        b_rows = keep.tile([P, P], F32, name="b_rows")
-        ident = keep.tile([P, P], F32, name="ident")
         bias = keep.tile([P, ROW_TILES], F32, name="bias")
         placed = [keep.tile([P, T], F32, name="placed%d" % m) for m in range(ROW_TILES)]
 
@@ -53,6 +49,7 @@ def tile_list_tabhs_d_bias_kernel(tc, tab, w4_words, w4_scales, c, u, b, wgo, of
         w_scales32 = w4_scales.bitcast(I32)
         u_rows = u.rearrange("(p j) n -> p j n", j=PACK)
 
+        w_rows = w4_words.bitcast(I32).rearrange("a p n -> p a n")
         nc.vector.memset(tab_planes[:], 0)
         nc.sync.dma_start(pick[:], offs)
         nc.sync.dma_start(tab_words[0][:], tab32[0, 0 : P * T].rearrange("(p t) -> p t", p=P))
@@ -62,25 +59,25 @@ def tile_list_tabhs_d_bias_kernel(tc, tab, w4_words, w4_scales, c, u, b, wgo, of
             rows = tab32[:, first + q * T : first + (q + 1) * T].rearrange("a (r t) -> r a t", r=4)
             nc.sync.dma_start(tab_planes[32 * q : 32 * q + 4, :, :], rows)
         nc.sync.dma_start(c_raw[:], c.rearrange("(p j) s -> p j s", j=PACK))
-        nc.sync.dma_start(u_raw0[:], u_rows[:, :, 0:P])
+        nc.sync.dma_start(u_raw01[:], u_rows[:, :, 0 : 2 * P])
         nc.sync.dma_start(tab_words[2][:], tab32[2, 0 : P * T].rearrange("(p t) -> p t", p=P))
-        nc.sync.dma_start(w_words[:].bitcast(I32), w4_words.bitcast(I32).rearrange("a p n -> p a n"))
         nc.vector.memset(w_planes[:], 0)
         for q in range(4):
             rows = w_scales32[:, 4 * q : 4 * q + 4, :].rearrange("a r n -> r a n")
             nc.sync.dma_start(w_planes[32 * q : 32 * q + 4, :, :], rows)
-        nc.sync.dma_start(u_raw1[:], u_rows[:, :, P : 2 * P])
+        nc.sync.dma_start(w_words[0][:].bitcast(I32), w_rows[:, :, 0 * P : 1 * P])
+        with nc.allow_non_contiguous_dma(reason="one bias value a partition"):
+            nc.sync.dma_start(bias[:], b.rearrange("(m p) -> p m", p=P))
+        nc.sync.dma_start(weights[:], wgo)
         nc.sync.dma_start(place[:], offs2)
         nc.sync.dma_start(u_raw23[:], u_rows[:, :, 2 * P : 4 * P])
-        make_identity(nc, ident[:])
-        nc.gpsimd.memset(b_rows[:], 0.0)
-        nc.gpsimd.dma_start(b_rows[0:ROW_TILES, :], b.rearrange("(m p) -> m p", p=P))
-        nc.gpsimd.dma_start(weights[:], wgo)
+        nc.sync.dma_start(w_words[1][:].bitcast(I32), w_rows[:, :, 1 * P : 2 * P])
         for m in range(ROW_TILES):
-            nc.vector.memset(placed[m][:], 0.0)
+            engine = nc.vector if m < 2 else nc.gpsimd
+            engine.memset(placed[m][:], 0.0)
 
-        def interleave(raw, width, name):
-            grouped = keep.tile([P, width, PACK], BF16, name=name, align_bytes=64)
+        def interleave(raw, width, name, tag):
+            grouped = keep.tile([P, width, PACK], BF16, name=name, tag=tag, align_bytes=64)
             nc.scalar.activation(
                 grouped[:].rearrange("p (w i) j -> p w j i", i=4),
                 raw.rearrange("p j (w i) -> p w j i", i=4),
@@ -89,7 +86,7 @@ def tile_list_tabhs_d_bias_kernel(tc, tab, w4_words, w4_scales, c, u, b, wgo, of
             return grouped
 
         def quantize(grouped, width, name):
-            codes = keep.tile([P, width], U32, name=name + "_codes", align_bytes=64)
+            codes = keep.tile([P, width], U32, name=name + "_codes", tag=name + "_codes", align_bytes=64)
             scales = keep.tile([P, width], U8, name=name + "_scales", align_bytes=64)
             nc.vector.quantize_mx(
                 out=codes[:].bitcast(FP8X4),
@@ -98,13 +95,9 @@ def tile_list_tabhs_d_bias_kernel(tc, tab, w4_words, w4_scales, c, u, b, wgo, of
             )
             return codes, scales
 
-        c_bf = [interleave(c_raw[:, :, 0:HALF], HALF, "c_bf0")]
-        u_bf = [interleave(u_raw0[:], P, "u_bf0")]
-        c_bf.append(interleave(c_raw[:, :, HALF:S], HALF, "c_bf1"))
-
-        b_t = psum.tile([P, P], F32, name="b_t", tag="bank7")
-        nc.tensor.transpose(b_t[:], b_rows[:], ident[:])
-        nc.scalar.activation(bias[:], b_t[:, 0:ROW_TILES], COPY)
+        c_bf = interleave(c_raw[:], S, "c_bf", "stage_c")
+        u_bf = [interleave(u_raw01[:, :, 0:P], P, "u_bf0", "stage_u0")]
+        u_bf.append(interleave(u_raw01[:, :, P : 2 * P], P, "u_bf1", "stage_u1"))
 
         got_scales = [keep.tile([P, S], U8, name="got_scales%d" % a, align_bytes=64) for a in range(PASSES)]
         got_words = [keep.tile([P, S], U32, name="got_words%d" % a, align_bytes=64) for a in range(PASSES)]
@@ -121,34 +114,33 @@ def tile_list_tabhs_d_bias_kernel(tc, tab, w4_words, w4_scales, c, u, b, wgo, of
         gather_words(1, 0, S)
         for a in range(PASSES):
             gather_scales(a, 0, S)
-        c_q = [quantize(c_bf[0], HALF, "c0")]
-        gather_words(2, 0, HALF)
+        c_q = quantize(c_bf, S, "c")
+        gather_words(2, 0, S)
         u_q = [quantize(u_bf[0], P, "u0")]
-        gather_words(2, HALF, S)
-        c_q.append(quantize(c_bf[1], HALF, "c1"))
+        u_q.append(quantize(u_bf[1], P, "u1"))
 
         def product(m, h):
             acc = psum.tile([P, HALF], F32, name="acc%d" % (2 * m + h), tag="bank%d" % (2 * m + h))
             cols = slice(h * HALF, (h + 1) * HALF)
+            for a in range(PASSES):
+                nc.tensor.matmul_mx(
+                    out=acc[:],
+                    lhsT=w_words[m // 2][:, a, 2 * P * (m % 2) : 2 * P * (m % 2 + 1)].bitcast(FP4X4),
+                    lhsT_scale=w_planes[:, a, :].bitcast(U8)[:, P * m : P * (m + 1)],
+                    rhs=got_words[a][:, cols].bitcast(FP8X4),
+                    rhs_scale=got_scales[a][:, cols],
+                    start=(a == 0),
+                    stop=False,
+                )
             nc.tensor.matmul_mx(
                 out=acc[:],
                 lhsT=u_q[m][0][:].bitcast(FP8X4),
                 lhsT_scale=u_q[m][1][:],
-                rhs=c_q[h][0][:].bitcast(FP8X4),
-                rhs_scale=c_q[h][1][:],
-                start=True,
-                stop=False,
+                rhs=c_q[0][:, cols].bitcast(FP8X4),
+                rhs_scale=c_q[1][:, cols],
+                start=False,
+                stop=True,
             )
-            for a in range(PASSES):
-                nc.tensor.matmul_mx(
-                    out=acc[:],
-                    lhsT=w_words[:, a, 2 * P * m : 2 * P * (m + 1)].bitcast(FP4X4),
-                    lhsT_scale=w_planes[:, a, :].bitcast(U8)[:, P * m : P * (m + 1)],
-                    rhs=got_words[a][:, cols].bitcast(FP8X4),
-                    rhs_scale=got_scales[a][:, cols],
-                    start=False,
-                    stop=(a == PASSES - 1),
-                )
             y = keep.tile([P, HALF], F32, name="y%d" % (2 * m + h))
             nc.scalar.activation(y[:], acc[:], IDENTITY, bias=bias[:, m : m + 1])
             return y
@@ -161,22 +153,20 @@ def tile_list_tabhs_d_bias_kernel(tc, tab, w4_words, w4_scales, c, u, b, wgo, of
             nc.sync.dma_start(out[m * P : (m + 1) * P, :], placed[m][:])
 
         y00 = product(0, 0)
+        y10 = product(1, 0)
         y01 = product(0, 1)
-        u_bf.append(interleave(u_raw1[:], P, "u_bf1"))
+        u_bf.append(interleave(u_raw23[:, :, 0:P], P, "u_bf2", "u0_codes"))
+        y11 = product(1, 1)
+        u_bf.append(interleave(u_raw23[:, :, P : 2 * P], P, "u_bf3", "u1_codes"))
         scatter(0, 0, y00)
-        u_q.append(quantize(u_bf[1], P, "u1"))
+        scatter(1, 0, y10)
         scatter(0, 1, y01)
         store(0)
-        y10 = product(1, 0)
-        y11 = product(1, 1)
-        u_bf.append(interleave(u_raw23[:, :, 0:P], P, "u_bf2"))
-        u_bf.append(interleave(u_raw23[:, :, P : 2 * P], P, "u_bf3"))
-        scatter(1, 0, y10)
         u_q.append(quantize(u_bf[2], P, "u2"))
+        y20 = product(2, 0)
         scatter(1, 1, y11)
         store(1)
         u_q.append(quantize(u_bf[3], P, "u3"))
-        y20 = product(2, 0)
         y30 = product(3, 0)
         y21 = product(2, 1)
         y31 = product(3, 1)

@@ -1,6 +1,7 @@
 from contextlib import ExitStack
 
 import concourse.mybir as mybir
+from concourse.masks import make_identity
 
 K, M, T, S = 1536, 512, 512, 256
 L = 512
@@ -43,7 +44,8 @@ def tile_list_tabhs_d_bias_kernel(tc, tab, w4_words, w4_scales, c, u, b, wgo, of
         u_raw23 = keep.tile([P, PACK, 2 * P], F32, name="u_raw23")
         weights = keep.tile([P, S], F32, name="weights")
         bias = keep.tile([P, ROW_TILES], F32, name="bias")
-        placed = [keep.tile([P, T], F32, name="placed%d" % m) for m in range(ROW_TILES)]
+        b_rows = keep.tile([P, P], F32, name="b_rows")
+        ident = keep.tile([P, P], F32, name="ident")
 
         tab32 = tab.bitcast(I32)
         w_scales32 = w4_scales.bitcast(I32)
@@ -66,15 +68,22 @@ def tile_list_tabhs_d_bias_kernel(tc, tab, w4_words, w4_scales, c, u, b, wgo, of
             rows = w_scales32[:, 4 * q : 4 * q + 4, :].rearrange("a r n -> r a n")
             nc.sync.dma_start(w_planes[32 * q : 32 * q + 4, :, :], rows)
         nc.sync.dma_start(w_words[0][:].bitcast(I32), w_rows[:, :, 0 * P : 1 * P])
-        with nc.allow_non_contiguous_dma(reason="one bias value a partition"):
-            nc.sync.dma_start(bias[:], b.rearrange("(m p) -> p m", p=P))
         nc.sync.dma_start(weights[:], wgo)
         nc.sync.dma_start(place[:], offs2)
         nc.sync.dma_start(u_raw23[:], u_rows[:, :, 2 * P : 4 * P])
         nc.sync.dma_start(w_words[1][:].bitcast(I32), w_rows[:, :, 1 * P : 2 * P])
-        for m in range(ROW_TILES):
-            engine = nc.vector if m < 2 else nc.gpsimd
-            engine.memset(placed[m][:], 0.0)
+        make_identity(nc, ident[:])
+        nc.gpsimd.memset(b_rows[:], 0.0)
+        nc.gpsimd.dma_start(b_rows[0:ROW_TILES, :], b.rearrange("(m p) -> m p", p=P))
+        placed = []
+
+        def clear(m, tag):
+            tile = keep.tile([P, T], F32, name="placed%d" % m, tag=tag, align_bytes=64)
+            nc.vector.memset(tile[:], 0.0)
+            placed.append(tile)
+
+        clear(0, "placed0")
+        clear(1, "placed1")
 
         def interleave(raw, width, name, tag):
             grouped = keep.tile([P, width, PACK], BF16, name=name, tag=tag, align_bytes=64)
@@ -94,6 +103,10 @@ def tile_list_tabhs_d_bias_kernel(tc, tab, w4_words, w4_scales, c, u, b, wgo, of
                 in_=grouped[:].rearrange("p w j -> p (w j)"),
             )
             return codes, scales
+
+        b_t = psum.tile([P, P], F32, name="b_t", tag="bank7")
+        nc.tensor.transpose(b_t[:], b_rows[:], ident[:])
+        nc.scalar.activation(bias[:], b_t[:, 0:ROW_TILES], COPY)
 
         c_bf = interleave(c_raw[:], S, "c_bf", "stage_c")
         u_bf = [interleave(u_raw01[:, :, 0:P], P, "u_bf0", "stage_u0")]
@@ -118,6 +131,8 @@ def tile_list_tabhs_d_bias_kernel(tc, tab, w4_words, w4_scales, c, u, b, wgo, of
         gather_words(2, 0, S)
         u_q = [quantize(u_bf[0], P, "u0")]
         u_q.append(quantize(u_bf[1], P, "u1"))
+        clear(2, "stage_u0")
+        clear(3, "stage_u1")
 
         def product(m, h):
             acc = psum.tile([P, HALF], F32, name="acc%d" % (2 * m + h), tag="bank%d" % (2 * m + h))

@@ -37,53 +37,49 @@ def tile_list_tabhs_d_bias_kernel(tc, tab, w4_words, w4_scales, c, u, b, wgo, of
         place = keep.tile([P, S // 16], U16, name="place")
         tab_planes = keep.tile([P, PASSES, T // 4], I32, name="tab_planes", align_bytes=64)
         w_planes = keep.tile([P, PASSES, M // 4], I32, name="w_planes", align_bytes=64)
-        tab_words = [keep.tile([P, T], I32, name="tab_words%d" % a, align_bytes=64) for a in range(PASSES)]
-        w_words = [keep.tile([P, PASSES, M], U8, name="w_words%d" % i, align_bytes=64) for i in range(2)]
-        c_raw = keep.tile([P, PACK, S], F32, name="c_raw")
-        u_raw01 = keep.tile([P, PACK, 2 * P], F32, name="u_raw01")
-        u_raw23 = keep.tile([P, PACK, 2 * P], F32, name="u_raw23")
+        tab_words = {}
+        c_raw = keep.tile([P, PACK, S], F32, name="c_raw", tag="c_raw", align_bytes=64)
         weights = keep.tile([P, S], F32, name="weights")
-        bias = keep.tile([P, ROW_TILES], F32, name="bias")
         b_rows = keep.tile([P, P], F32, name="b_rows")
         ident = keep.tile([P, P], F32, name="ident")
+        placed = [keep.tile([P, T], F32, name="placed%d" % m, align_bytes=64) for m in range(ROW_TILES)]
 
         tab32 = tab.bitcast(I32)
         w_scales32 = w4_scales.bitcast(I32)
         u_rows = u.rearrange("(p j) n -> p j n", j=PACK)
-
         w_rows = w4_words.bitcast(I32).rearrange("a p n -> p a n")
-        nc.vector.memset(tab_planes[:], 0)
-        nc.sync.dma_start(pick[:], offs)
-        nc.sync.dma_start(tab_words[0][:], tab32[0, 0 : P * T].rearrange("(p t) -> p t", p=P))
-        nc.sync.dma_start(tab_words[1][:], tab32[1, 0 : P * T].rearrange("(p t) -> p t", p=P))
-        first = P * T
-        for q in range(4):
-            rows = tab32[:, first + q * T : first + (q + 1) * T].rearrange("a (r t) -> r a t", r=4)
-            nc.sync.dma_start(tab_planes[32 * q : 32 * q + 4, :, :], rows)
-        nc.sync.dma_start(c_raw[:], c.rearrange("(p j) s -> p j s", j=PACK))
-        nc.sync.dma_start(u_raw01[:], u_rows[:, :, 0 : 2 * P])
-        nc.sync.dma_start(tab_words[2][:], tab32[2, 0 : P * T].rearrange("(p t) -> p t", p=P))
-        nc.vector.memset(w_planes[:], 0)
-        for q in range(4):
-            rows = w_scales32[:, 4 * q : 4 * q + 4, :].rearrange("a r n -> r a n")
-            nc.sync.dma_start(w_planes[32 * q : 32 * q + 4, :, :], rows)
-        nc.sync.dma_start(w_words[0][:].bitcast(I32), w_rows[:, :, 0 * P : 1 * P])
-        nc.sync.dma_start(weights[:], wgo)
-        nc.sync.dma_start(place[:], offs2)
-        nc.sync.dma_start(u_raw23[:], u_rows[:, :, 2 * P : 4 * P])
-        nc.sync.dma_start(w_words[1][:].bitcast(I32), w_rows[:, :, 1 * P : 2 * P])
-        make_identity(nc, ident[:])
-        nc.gpsimd.memset(b_rows[:], 0.0)
-        nc.gpsimd.dma_start(b_rows[0:ROW_TILES, :], b.rearrange("(m p) -> m p", p=P))
-        placed = []
+        u_raw = {}
+        w_words = {}
 
-        def clear(m, tag):
-            tile = keep.tile([P, T], F32, name="placed%d" % m, tag=tag, align_bytes=64)
-            nc.vector.memset(tile[:], 0.0)
-            placed.append(tile)
+        def load_table(lo, hi):
+            tile = keep.tile([P, (hi - lo) * T], I32, name="tab_words%d" % lo, align_bytes=64)
+            rows = tab32[lo:hi, 0 : P * T].rearrange("a (p t) -> p a t", p=P)
+            nc.sync.dma_start(tile[:].rearrange("p (a t) -> p a t", t=T), rows)
+            for a in range(lo, hi):
+                tab_words[a] = tile[:, (a - lo) * T : (a - lo + 1) * T]
 
-        clear(0, "placed0")
-        clear(1, "placed1")
+        def load_table_scales(eng):
+            first = P * T
+            for q in range(4):
+                rows = tab32[:, first + q * T : first + (q + 1) * T].rearrange("a (r t) -> r a t", r=4)
+                eng.dma_start(tab_planes[32 * q : 32 * q + 4, :, :], rows)
+
+        def load_w_scales(eng):
+            for q in range(4):
+                rows = w_scales32[:, 4 * q : 4 * q + 4, :].rearrange("a r n -> r a n")
+                eng.dma_start(w_planes[32 * q : 32 * q + 4, :, :], rows)
+
+        def load_u(lo, hi):
+            tile = keep.tile([P, PACK, (hi - lo) * P], F32, name="u_raw%d" % lo, tag="u_raw%d" % lo, align_bytes=64)
+            nc.sync.dma_start(tile[:], u_rows[:, :, lo * P : hi * P])
+            for m in range(lo, hi):
+                u_raw[m] = tile[:, :, (m - lo) * P : (m - lo + 1) * P]
+
+        def load_w(lo, hi):
+            tile = keep.tile([P, PASSES, (hi - lo) * 2 * P], U8, name="w_words%d" % lo, align_bytes=64)
+            nc.sync.dma_start(tile[:].bitcast(I32), w_rows[:, :, lo * P // 2 : hi * P // 2])
+            for m in range(lo, hi):
+                w_words[m] = [tile[:, a, (m - lo) * 2 * P : (m - lo + 1) * 2 * P] for a in range(PASSES)]
 
         def interleave(raw, width, name, tag):
             grouped = keep.tile([P, width, PACK], BF16, name=name, tag=tag, align_bytes=64)
@@ -96,7 +92,7 @@ def tile_list_tabhs_d_bias_kernel(tc, tab, w4_words, w4_scales, c, u, b, wgo, of
 
         def quantize(grouped, width, name):
             codes = keep.tile([P, width], U32, name=name + "_codes", tag=name + "_codes", align_bytes=64)
-            scales = keep.tile([P, width], U8, name=name + "_scales", align_bytes=64)
+            scales = keep.tile([P, width], U8, name=name + "_scales", tag=name + "_scales", align_bytes=64)
             nc.vector.quantize_mx(
                 out=codes[:].bitcast(FP8X4),
                 scales=scales[:],
@@ -104,90 +100,154 @@ def tile_list_tabhs_d_bias_kernel(tc, tab, w4_words, w4_scales, c, u, b, wgo, of
             )
             return codes, scales
 
-        b_t = psum.tile([P, P], F32, name="b_t", tag="bank7")
-        nc.tensor.transpose(b_t[:], b_rows[:], ident[:])
-        nc.scalar.activation(bias[:], b_t[:, 0:ROW_TILES], COPY)
+        c_codes = keep.tile([P, S], U32, name="c_codes", align_bytes=64)
+        c_scales = keep.tile([P, S], U8, name="c_scales", align_bytes=64)
 
-        c_bf = interleave(c_raw[:], S, "c_bf", "stage_c")
-        u_bf = [interleave(u_raw01[:, :, 0:P], P, "u_bf0", "stage_u0")]
-        u_bf.append(interleave(u_raw01[:, :, P : 2 * P], P, "u_bf1", "stage_u1"))
+        def quantize_c(grouped, lo, hi):
+            nc.vector.quantize_mx(
+                out=c_codes[:, lo:hi].bitcast(FP8X4),
+                scales=c_scales[:, lo:hi],
+                in_=grouped[:].rearrange("p w j -> p (w j)"),
+            )
 
         got_scales = [keep.tile([P, S], U8, name="got_scales%d" % a, align_bytes=64) for a in range(PASSES)]
-        got_words = [keep.tile([P, S], U32, name="got_words%d" % a, align_bytes=64) for a in range(PASSES)]
+        got_words = {}
+
+        def words_tile(lo, hi, tag):
+            tile = keep.tile([P, (hi - lo) * S], U32, name="got_words%d" % lo, tag=tag, align_bytes=64)
+            for a in range(lo, hi):
+                got_words[a] = tile[:, (a - lo) * S : (a - lo + 1) * S]
 
         def gather_scales(a, lo, hi):
             window = tab_planes[:, a, :].bitcast(U8)
             nc.vector.tensor_copy(got_scales[a][:, lo:hi], window.indirect(pick[:, lo // 16 : hi // 16]))
 
         def gather_words(a, lo, hi):
-            window = tab_words[a][:].bitcast(U32)
+            window = tab_words[a].bitcast(U32)
             nc.vector.tensor_copy(got_words[a][:, lo:hi], window.indirect(pick[:, lo // 16 : hi // 16]))
 
-        gather_words(0, 0, S)
-        gather_words(1, 0, S)
-        for a in range(PASSES):
-            gather_scales(a, 0, S)
-        c_q = quantize(c_bf, S, "c")
-        gather_words(2, 0, S)
-        u_q = [quantize(u_bf[0], P, "u0")]
-        u_q.append(quantize(u_bf[1], P, "u1"))
-        clear(2, "stage_u0")
-        clear(3, "stage_u1")
+        u_q = {}
+        u_bf = {}
 
-        def product(m, h):
-            acc = psum.tile([P, HALF], F32, name="acc%d" % (2 * m + h), tag="bank%d" % (2 * m + h))
-            cols = slice(h * HALF, (h + 1) * HALF)
-            for a in range(PASSES):
-                nc.tensor.matmul_mx(
-                    out=acc[:],
-                    lhsT=w_words[m // 2][:, a, 2 * P * (m % 2) : 2 * P * (m % 2 + 1)].bitcast(FP4X4),
-                    lhsT_scale=w_planes[:, a, :].bitcast(U8)[:, P * m : P * (m + 1)],
-                    rhs=got_words[a][:, cols].bitcast(FP8X4),
-                    rhs_scale=got_scales[a][:, cols],
-                    start=(a == 0),
-                    stop=False,
-                )
+        def table_pass(acc, m, a, lo, first, last, base):
+            nc.tensor.matmul_mx(
+                out=acc[:, lo - base : lo - base + HALF],
+                lhsT=w_words[m][a].bitcast(FP4X4),
+                lhsT_scale=w_planes[:, a, :].bitcast(U8)[:, P * m : P * (m + 1)],
+                rhs=got_words[a][:, lo : lo + HALF].bitcast(FP8X4),
+                rhs_scale=got_scales[a][:, lo : lo + HALF],
+                start=first,
+                stop=last,
+            )
+
+        def dense_pass(acc, m, lo, hi, first, last):
             nc.tensor.matmul_mx(
                 out=acc[:],
                 lhsT=u_q[m][0][:].bitcast(FP8X4),
                 lhsT_scale=u_q[m][1][:],
-                rhs=c_q[0][:, cols].bitcast(FP8X4),
-                rhs_scale=c_q[1][:, cols],
-                start=False,
-                stop=True,
+                rhs=c_codes[:, lo:hi].bitcast(FP8X4),
+                rhs_scale=c_scales[:, lo:hi],
+                start=first,
+                stop=last,
             )
-            y = keep.tile([P, HALF], F32, name="y%d" % (2 * m + h))
-            nc.scalar.activation(y[:], acc[:], IDENTITY, bias=bias[:, m : m + 1])
-            return y
 
-        def scatter(m, h, y):
-            offsets = place[:, h * HALF // 16 : (h + 1) * HALF // 16]
-            nc.vector.tensor_tensor(placed[m][:].indirect(offsets), y[:], weights[:, h * HALF : (h + 1) * HALF], MULT)
+        def product(m, lo, hi, bank, dense_at):
+            acc = psum.tile([P, hi - lo], F32, name="acc%d_%d" % (m, lo), tag="bank%d" % bank)
+            steps = [(a, x) for a in range(PASSES) for x in range(lo, hi, HALF)]
+            steps.insert(dense_at * (hi - lo) // HALF, None)
+            for n, step in enumerate(steps):
+                if step is None:
+                    dense_pass(acc, m, lo, hi, n == 0, n == len(steps) - 1)
+                else:
+                    table_pass(acc, m, step[0], step[1], n == 0, n == len(steps) - 1, lo)
+            return acc
+
+        y = {}
+
+        def y_tile(m, tag):
+            y[m] = keep.tile([P, S], F32, name="y%d" % m, tag=tag, align_bytes=64)
+
+        def evacuate(acc, m, lo, hi):
+            nc.scalar.activation(y[m][:, lo:hi], acc[:], IDENTITY, bias=bias[:, m : m + 1])
+
+        def scatter(m, lo, hi):
+            nc.vector.tensor_tensor(placed[m][:].indirect(place[:, lo // 16 : hi // 16]), y[m][:, lo:hi], weights[:, lo:hi], MULT)
 
         def store(m):
             nc.sync.dma_start(out[m * P : (m + 1) * P, :], placed[m][:])
 
-        y00 = product(0, 0)
-        y10 = product(1, 0)
-        y01 = product(0, 1)
-        u_bf.append(interleave(u_raw23[:, :, 0:P], P, "u_bf2", "u0_codes"))
-        y11 = product(1, 1)
-        u_bf.append(interleave(u_raw23[:, :, P : 2 * P], P, "u_bf3", "u1_codes"))
-        scatter(0, 0, y00)
-        scatter(1, 0, y10)
-        scatter(0, 1, y01)
+        nc.gpsimd.memset(tab_planes[:], 0)
+        nc.vector.memset(w_planes[:], 0)
+        nc.sync.dma_start(pick[:], offs)
+        load_table(0, 1)
+        load_table_scales(nc.sync)
+        nc.sync.dma_start(c_raw[:], c.rearrange("(p j) s -> p j s", j=PACK))
+        load_u(0, 1)
+        load_table(1, 3)
+        load_w(0, 2)
+        load_w_scales(nc.sync)
+        load_u(1, 2)
+        nc.sync.dma_start(weights[:], wgo)
+        nc.sync.dma_start(place[:], offs2)
+        load_u(2, 3)
+        load_w(2, 4)
+        load_u(3, 4)
+        nc.gpsimd.memset(b_rows[:], 0.0)
+        nc.gpsimd.dma_start(b_rows[0:ROW_TILES, :], b.rearrange("(m p) -> m p", p=P))
+        make_identity(nc, ident[:])
+        nc.vector.memset(placed[0][:], 0.0)
+        nc.vector.memset(placed[1][:], 0.0)
+        nc.gpsimd.memset(placed[2][:], 0.0)
+        nc.gpsimd.memset(placed[3][:], 0.0)
+
+        b_t = psum.tile([P, P], F32, name="b_t", tag="bank7")
+        nc.tensor.transpose(b_t[:], b_rows[:], ident[:])
+        c_bf0 = interleave(c_raw[:, :, 0:HALF], HALF, "c_bf0", "stage_c0")
+        u_bf[0] = interleave(u_raw[0], P, "u_bf0", "stage_u0")
+        c_bf1 = interleave(c_raw[:, :, HALF:S], HALF, "c_bf1", "stage_c1")
+        bias = keep.tile([P, ROW_TILES], F32, name="bias", tag="c_raw", align_bytes=64)
+        nc.scalar.activation(bias[:], b_t[:, 0:ROW_TILES], COPY)
+        u_bf[1] = interleave(u_raw[1], P, "u_bf1", "stage_u1")
+
+        words_tile(0, 1, "got_words0")
+        gather_words(0, 0, S)
+        for a in range(PASSES):
+            gather_scales(a, 0, S)
+        quantize_c(c_bf0, 0, HALF)
+        u_q[0] = quantize(u_bf[0], P, "u0")
+        words_tile(1, 3, "stage_u0")
+        gather_words(1, 0, HALF)
+        gather_words(2, 0, HALF)
+        acc0a = product(0, 0, HALF, 0, 0)
+        y_tile(0, "y0")
+        evacuate(acc0a, 0, 0, HALF)
+        quantize_c(c_bf1, HALF, S)
+        gather_words(1, HALF, S)
+        gather_words(2, HALF, S)
+        acc0b = product(0, HALF, S, 1, 3)
+        evacuate(acc0b, 0, HALF, S)
+        u_q[1] = quantize(u_bf[1], P, "u1")
+        u_bf[2] = interleave(u_raw[2], P, "u_bf2", "u0_codes")
+        scatter(0, 0, HALF)
+        acc1a = product(1, 0, HALF, 0, 3)
+        acc1b = product(1, HALF, S, 1, 3)
+        y_tile(1, "u_raw2")
+        evacuate(acc1a, 1, 0, HALF)
+        evacuate(acc1b, 1, HALF, S)
+        scatter(0, HALF, S)
         store(0)
-        u_q.append(quantize(u_bf[2], P, "u2"))
-        y20 = product(2, 0)
-        scatter(1, 1, y11)
+        u_q[2] = quantize(u_bf[2], P, "u2")
+        u_bf[3] = interleave(u_raw[3], P, "u_bf3", "u1_codes")
+        scatter(1, 0, S)
         store(1)
-        u_q.append(quantize(u_bf[3], P, "u3"))
-        y30 = product(3, 0)
-        y21 = product(2, 1)
-        y31 = product(3, 1)
-        scatter(2, 0, y20)
-        scatter(3, 0, y30)
-        scatter(2, 1, y21)
+        u_q[3] = quantize(u_bf[3], P, "u3")
+        acc2 = product(2, 0, S, 0, 3)
+        y_tile(2, "u_raw3")
+        evacuate(acc2, 2, 0, S)
+        acc3 = product(3, 0, S, 1, 3)
+        y_tile(3, "y3")
+        evacuate(acc3, 3, 0, S)
+        scatter(2, 0, S)
         store(2)
-        scatter(3, 1, y31)
+        scatter(3, 0, S)
         store(3)

@@ -60,14 +60,14 @@ def tile_list_tabhs_d_bias_kernel(tc, tab, w4_words, w4_scales, c, u, b, wgo, of
 
         def load_table_scales(eng):
             first = P * T
-            for q in range(4):
-                rows = tab32[:, first + q * T : first + (q + 1) * T].rearrange("a (r t) -> r a t", r=4)
-                eng.dma_start(tab_planes[32 * q : 32 * q + 4, :, :], rows)
+            rows = tab32[:, first : first + 4 * T].rearrange("a (q r t) -> r q a t", q=4, r=4)
+            for r in range(4):
+                eng.dma_start(tab_planes[r:P:32, :, :], rows[r])
 
         def load_w_scales(eng):
-            for q in range(4):
-                rows = w_scales32[:, 4 * q : 4 * q + 4, :].rearrange("a r n -> r a n")
-                eng.dma_start(w_planes[32 * q : 32 * q + 4, :, :], rows)
+            rows = w_scales32.rearrange("a (q r) n -> r q a n", r=4)
+            for r in range(4):
+                eng.dma_start(w_planes[r:P:32, :, :], rows[r])
 
         def load_u(lo, hi):
             tile = keep.tile([P, PACK, (hi - lo) * P], F32, name="u_raw%d" % lo, tag="u_raw%d" % lo, align_bytes=64)
@@ -178,8 +178,8 @@ def tile_list_tabhs_d_bias_kernel(tc, tab, w4_words, w4_scales, c, u, b, wgo, of
 
         nc.gpsimd.memset(tab_planes[:], 0)
         nc.vector.memset(w_planes[:], 0)
-        nc.sync.dma_start(pick[:], offs)
         load_table(0, 1)
+        nc.sync.dma_start(pick[:], offs)
         load_table_scales(nc.sync)
         nc.sync.dma_start(c_raw[:], c.rearrange("(p j) s -> p j s", j=PACK))
         load_u(0, 1)

@@ -164,20 +164,23 @@ def tile_list_tabhs_d_bias_kernel(tc, tab, w4_words, w4_scales, c, u, b, wgo, of
 
         y = {}
 
-        def y_tile(m, tag):
-            y[m] = keep.tile([P, S], F32, name="y%d" % m, tag=tag, align_bytes=64)
+        def y_tile(m, lo, hi, tag):
+            tile = keep.tile([P, hi - lo], F32, name="y%d_%d" % (m, lo), tag=tag, align_bytes=64)
+            y[m, lo, hi] = tile[:]
+            for x in range(lo, hi, HALF):
+                y[m, x, x + HALF] = tile[:, x - lo : x - lo + HALF]
 
-        def evacuate(acc, m, lo, hi):
-            nc.scalar.activation(y[m][:, lo:hi], acc[:], IDENTITY, bias=bias[:, m : m + 1])
+        def evacuate(acc, m, lo, hi, column):
+            nc.scalar.activation(y[m, lo, hi], acc[:], IDENTITY, bias=column)
 
         def scatter(m, lo, hi):
-            nc.vector.tensor_tensor(placed[m][:].indirect(place[:, lo // 16 : hi // 16]), y[m][:, lo:hi], weights[:, lo:hi], MULT)
+            nc.vector.tensor_tensor(placed[m][:].indirect(place[:, lo // 16 : hi // 16]), y[m, lo, hi], weights[:, lo:hi], MULT)
 
         def store(m):
             nc.sync.dma_start(out[m * P : (m + 1) * P, :], placed[m][:])
 
         nc.gpsimd.memset(tab_planes[:], 0)
-        nc.vector.memset(w_planes[:], 0)
+        nc.gpsimd.memset(w_planes[:], 0)
         load_table(0, 1)
         nc.sync.dma_start(pick[:], offs)
         load_table_scales(nc.sync)
@@ -187,18 +190,18 @@ def tile_list_tabhs_d_bias_kernel(tc, tab, w4_words, w4_scales, c, u, b, wgo, of
         load_w(0, 2)
         load_w_scales(nc.sync)
         load_u(1, 2)
-        nc.sync.dma_start(weights[:], wgo)
         nc.sync.dma_start(place[:], offs2)
         load_u(2, 3)
         load_w(2, 4)
         load_u(3, 4)
         nc.gpsimd.memset(b_rows[:], 0.0)
         nc.gpsimd.dma_start(b_rows[0:ROW_TILES, :], b.rearrange("(m p) -> m p", p=P))
+        nc.gpsimd.dma_start(weights[:], wgo)
         make_identity(nc, ident[:])
         nc.vector.memset(placed[0][:], 0.0)
         nc.vector.memset(placed[1][:], 0.0)
-        nc.gpsimd.memset(placed[2][:], 0.0)
-        nc.gpsimd.memset(placed[3][:], 0.0)
+        nc.vector.memset(placed[2][:], 0.0)
+        nc.vector.memset(placed[3][:], 0.0)
 
         b_t = psum.tile([P, P], F32, name="b_t", tag="bank7")
         nc.tensor.transpose(b_t[:], b_rows[:], ident[:])
@@ -219,21 +222,20 @@ def tile_list_tabhs_d_bias_kernel(tc, tab, w4_words, w4_scales, c, u, b, wgo, of
         gather_words(1, 0, HALF)
         gather_words(2, 0, HALF)
         acc0a = product(0, 0, HALF, 0, 0)
-        y_tile(0, "y0")
-        evacuate(acc0a, 0, 0, HALF)
+        y_tile(0, 0, HALF, "y0")
+        evacuate(acc0a, 0, 0, HALF, bias[:, 0:1])
         quantize_c(c_bf1, HALF, S)
         gather_words(1, HALF, S)
         gather_words(2, HALF, S)
         acc0b = product(0, HALF, S, 1, 3)
-        evacuate(acc0b, 0, HALF, S)
+        y_tile(0, HALF, S, "y0b")
+        evacuate(acc0b, 0, HALF, S, bias[:, 0:1])
         u_q[1] = quantize(u_bf[1], P, "u1")
-        u_bf[2] = interleave(u_raw[2], P, "u_bf2", "u0_codes")
         scatter(0, 0, HALF)
-        acc1a = product(1, 0, HALF, 0, 3)
-        acc1b = product(1, HALF, S, 1, 3)
-        y_tile(1, "u_raw2")
-        evacuate(acc1a, 1, 0, HALF)
-        evacuate(acc1b, 1, HALF, S)
+        u_bf[2] = interleave(u_raw[2], P, "u_bf2", "u0_codes")
+        acc1 = product(1, 0, S, 0, 3)
+        y_tile(1, 0, S, "u_raw2")
+        evacuate(acc1, 1, 0, S, bias[:, 1:2])
         scatter(0, HALF, S)
         store(0)
         u_q[2] = quantize(u_bf[2], P, "u2")
@@ -241,12 +243,12 @@ def tile_list_tabhs_d_bias_kernel(tc, tab, w4_words, w4_scales, c, u, b, wgo, of
         scatter(1, 0, S)
         store(1)
         u_q[3] = quantize(u_bf[3], P, "u3")
-        acc2 = product(2, 0, S, 0, 3)
-        y_tile(2, "u_raw3")
-        evacuate(acc2, 2, 0, S)
-        acc3 = product(3, 0, S, 1, 3)
-        y_tile(3, "y3")
-        evacuate(acc3, 3, 0, S)
+        acc2 = product(2, 0, S, 1, 3)
+        y_tile(2, 0, S, "u_raw3")
+        evacuate(acc2, 2, 0, S, bias[:, 2:3])
+        acc3 = product(3, 0, S, 0, 3)
+        y_tile(3, 0, S, "y3")
+        evacuate(acc3, 3, 0, S, bias[:, 3:4])
         scatter(2, 0, S)
         store(2)
         scatter(3, 0, S)

@@ -42,7 +42,11 @@ def tile_list_tabhs_d_bias_kernel(tc, tab, w4_words, w4_scales, c, u, b, wgo, of
         weights = keep.tile([P, S], F32, name="weights")
         b_rows = keep.tile([P, P], F32, name="b_rows")
         ident = keep.tile([P, P], F32, name="ident")
-        placed = [keep.tile([P, T], F32, name="placed%d" % m, align_bytes=64) for m in range(ROW_TILES)]
+        placed = {}
+
+        def clear(m, tag, eng):
+            placed[m] = keep.tile([P, T], F32, name="placed%d" % m, tag=tag, align_bytes=64)
+            eng.memset(placed[m][:], 0.0)
 
         tab32 = tab.bitcast(I32)
         w_scales32 = w4_scales.bitcast(I32)
@@ -180,43 +184,39 @@ def tile_list_tabhs_d_bias_kernel(tc, tab, w4_words, w4_scales, c, u, b, wgo, of
             nc.sync.dma_start(out[m * P : (m + 1) * P, :], placed[m][:])
 
         nc.gpsimd.memset(tab_planes[:], 0)
-        nc.gpsimd.memset(w_planes[:], 0)
+        nc.vector.memset(w_planes[:], 0)
         load_table(0, 1)
         nc.sync.dma_start(pick[:], offs)
         load_table_scales(nc.sync)
         nc.sync.dma_start(c_raw[:], c.rearrange("(p j) s -> p j s", j=PACK))
-        load_u(0, 1)
+        load_u(0, 2)
         load_table(1, 3)
         load_w(0, 2)
         load_w_scales(nc.sync)
-        load_u(1, 2)
+        nc.sync.dma_start(weights[:], wgo)
         nc.sync.dma_start(place[:], offs2)
         load_u(2, 3)
         load_w(2, 4)
         load_u(3, 4)
         nc.gpsimd.memset(b_rows[:], 0.0)
         nc.gpsimd.dma_start(b_rows[0:ROW_TILES, :], b.rearrange("(m p) -> m p", p=P))
-        nc.gpsimd.dma_start(weights[:], wgo)
         make_identity(nc, ident[:])
-        nc.vector.memset(placed[0][:], 0.0)
-        nc.vector.memset(placed[1][:], 0.0)
-        nc.vector.memset(placed[2][:], 0.0)
-        nc.vector.memset(placed[3][:], 0.0)
+        clear(0, "placed0", nc.vector)
+        clear(1, "placed1", nc.vector)
 
         b_t = psum.tile([P, P], F32, name="b_t", tag="bank7")
         nc.tensor.transpose(b_t[:], b_rows[:], ident[:])
-        c_bf0 = interleave(c_raw[:, :, 0:HALF], HALF, "c_bf0", "stage_c0")
+        c_bf = interleave(c_raw[:], S, "c_bf", "stage_c")
         u_bf[0] = interleave(u_raw[0], P, "u_bf0", "stage_u0")
-        c_bf1 = interleave(c_raw[:, :, HALF:S], HALF, "c_bf1", "stage_c1")
-        bias = keep.tile([P, ROW_TILES], F32, name="bias", tag="c_raw", align_bytes=64)
-        nc.scalar.activation(bias[:], b_t[:, 0:ROW_TILES], COPY)
         u_bf[1] = interleave(u_raw[1], P, "u_bf1", "stage_u1")
+        bias = keep.tile([P, ROW_TILES], F32, name="bias", tag="u_raw0", align_bytes=64)
+        nc.scalar.activation(bias[:], b_t[:, 0:ROW_TILES], COPY)
 
         words_tile(0, 1, "got_words0")
         gather_words(0, 0, S)
         for a in range(PASSES):
             gather_scales(a, 0, S)
-        quantize_c(c_bf0, 0, HALF)
+        quantize_c(c_bf, 0, S)
         u_q[0] = quantize(u_bf[0], P, "u0")
         words_tile(1, 3, "stage_u0")
         gather_words(1, 0, HALF)
@@ -224,13 +224,13 @@ def tile_list_tabhs_d_bias_kernel(tc, tab, w4_words, w4_scales, c, u, b, wgo, of
         acc0a = product(0, 0, HALF, 0, 0)
         y_tile(0, 0, HALF, "y0")
         evacuate(acc0a, 0, 0, HALF, bias[:, 0:1])
-        quantize_c(c_bf1, HALF, S)
         gather_words(1, HALF, S)
         gather_words(2, HALF, S)
         acc0b = product(0, HALF, S, 1, 3)
         y_tile(0, HALF, S, "y0b")
         evacuate(acc0b, 0, HALF, S, bias[:, 0:1])
         u_q[1] = quantize(u_bf[1], P, "u1")
+        clear(2, "stage_u1", nc.gpsimd)
         scatter(0, 0, HALF)
         u_bf[2] = interleave(u_raw[2], P, "u_bf2", "u0_codes")
         acc1 = product(1, 0, S, 0, 3)
@@ -239,6 +239,7 @@ def tile_list_tabhs_d_bias_kernel(tc, tab, w4_words, w4_scales, c, u, b, wgo, of
         scatter(0, HALF, S)
         store(0)
         u_q[2] = quantize(u_bf[2], P, "u2")
+        clear(3, "u0_codes", nc.gpsimd)
         u_bf[3] = interleave(u_raw[3], P, "u_bf3", "u1_codes")
         scatter(1, 0, S)
         store(1)

@@ -55,22 +55,22 @@ def tile_list_tabhs_d_bias_kernel(tc, tab, w4_words, w4_scales, c, u, b, wgo, of
         u_raw = {}
         w_words = {}
 
-        def load_table(lo, hi):
+        def load_table(lo, hi, eng):
             tile = keep.tile([P, (hi - lo) * T], I32, name="tab_words%d" % lo, align_bytes=64)
             rows = tab32[lo:hi, 0 : P * T].rearrange("a (p t) -> p a t", p=P)
-            nc.sync.dma_start(tile[:].rearrange("p (a t) -> p a t", t=T), rows)
+            eng.dma_start(tile[:].rearrange("p (a t) -> p a t", t=T), rows)
             for a in range(lo, hi):
                 tab_words[a] = tile[:, (a - lo) * T : (a - lo + 1) * T]
 
-        def load_table_scales(eng):
+        def load_table_scales(engines):
             first = P * T
             rows = tab32[:, first : first + 4 * T].rearrange("a (q r t) -> r q a t", q=4, r=4)
             for r in range(4):
-                eng.dma_start(tab_planes[r:P:32, :, :], rows[r])
+                engines[r].dma_start(tab_planes[r:P:32, :, :], rows[r])
 
-        def load_w_scales(eng):
+        def load_w_scales(eng, lo, hi):
             rows = w_scales32.rearrange("a (q r) n -> r q a n", r=4)
-            for r in range(4):
+            for r in range(lo, hi):
                 eng.dma_start(w_planes[r:P:32, :, :], rows[r])
 
         def load_u(lo, hi):
@@ -117,18 +117,17 @@ def tile_list_tabhs_d_bias_kernel(tc, tab, w4_words, w4_scales, c, u, b, wgo, of
         got_scales = [keep.tile([P, S], U8, name="got_scales%d" % a, align_bytes=64) for a in range(PASSES)]
         got_words = {}
 
-        def words_tile(lo, hi, tag):
-            tile = keep.tile([P, (hi - lo) * S], U32, name="got_words%d" % lo, tag=tag, align_bytes=64)
-            for a in range(lo, hi):
-                got_words[a] = tile[:, (a - lo) * S : (a - lo + 1) * S]
 
         def gather_scales(a, lo, hi):
             window = tab_planes[:, a, :].bitcast(U8)
             nc.vector.tensor_copy(got_scales[a][:, lo:hi], window.indirect(pick[:, lo // 16 : hi // 16]))
 
-        def gather_words(a, lo, hi):
+        def gather_words(a, lo, hi, tag):
+            tile = keep.tile([P, hi - lo], U32, name="got_words%d_%d" % (a, lo), tag=tag, align_bytes=64)
             window = tab_words[a].bitcast(U32)
-            nc.vector.tensor_copy(got_words[a][:, lo:hi], window.indirect(pick[:, lo // 16 : hi // 16]))
+            nc.vector.tensor_copy(tile[:], window.indirect(pick[:, lo // 16 : hi // 16]))
+            for x in range(lo, hi, HALF):
+                got_words[a, x] = tile[:, x - lo : x - lo + HALF]
 
         u_q = {}
         u_bf = {}
@@ -138,7 +137,7 @@ def tile_list_tabhs_d_bias_kernel(tc, tab, w4_words, w4_scales, c, u, b, wgo, of
                 out=acc[:, lo - base : lo - base + HALF],
                 lhsT=w_words[m][a].bitcast(FP4X4),
                 lhsT_scale=w_planes[:, a, :].bitcast(U8)[:, P * m : P * (m + 1)],
-                rhs=got_words[a][:, lo : lo + HALF].bitcast(FP8X4),
+                rhs=got_words[a, lo].bitcast(FP8X4),
                 rhs_scale=got_scales[a][:, lo : lo + HALF],
                 start=first,
                 stop=last,
@@ -185,14 +184,16 @@ def tile_list_tabhs_d_bias_kernel(tc, tab, w4_words, w4_scales, c, u, b, wgo, of
 
         nc.gpsimd.memset(tab_planes[:], 0)
         nc.vector.memset(w_planes[:], 0)
-        load_table(0, 1)
+        load_table(0, 1, nc.sync)
         nc.sync.dma_start(pick[:], offs)
-        load_table_scales(nc.sync)
+        load_table_scales([nc.sync] * 4)
         nc.sync.dma_start(c_raw[:], c.rearrange("(p j) s -> p j s", j=PACK))
-        load_u(0, 2)
-        load_table(1, 3)
+        load_table(1, 3, nc.sync)
+        load_w_scales(nc.sync, 0, 1)
+        load_u(0, 1)
         load_w(0, 2)
-        load_w_scales(nc.sync)
+        load_w_scales(nc.sync, 1, 4)
+        load_u(1, 2)
         nc.sync.dma_start(weights[:], wgo)
         nc.sync.dma_start(place[:], offs2)
         load_u(2, 3)
@@ -208,26 +209,22 @@ def tile_list_tabhs_d_bias_kernel(tc, tab, w4_words, w4_scales, c, u, b, wgo, of
         nc.tensor.transpose(b_t[:], b_rows[:], ident[:])
         c_bf = interleave(c_raw[:], S, "c_bf", "stage_c")
         u_bf[0] = interleave(u_raw[0], P, "u_bf0", "stage_u0")
-        u_bf[1] = interleave(u_raw[1], P, "u_bf1", "stage_u1")
         bias = keep.tile([P, ROW_TILES], F32, name="bias", tag="u_raw0", align_bytes=64)
         nc.scalar.activation(bias[:], b_t[:, 0:ROW_TILES], COPY)
+        u_bf[1] = interleave(u_raw[1], P, "u_bf1", "stage_u1")
 
-        words_tile(0, 1, "got_words0")
-        gather_words(0, 0, S)
+        gather_words(0, 0, S, "words0")
         for a in range(PASSES):
             gather_scales(a, 0, S)
+        gather_words(1, 0, S, "words1")
+        gather_words(2, 0, HALF, "words2")
         quantize_c(c_bf, 0, S)
         u_q[0] = quantize(u_bf[0], P, "u0")
-        words_tile(1, 3, "stage_u0")
-        gather_words(1, 0, HALF)
-        gather_words(2, 0, HALF)
-        acc0a = product(0, 0, HALF, 0, 0)
-        y_tile(0, 0, HALF, "y0")
+        acc0a = product(0, 0, HALF, 0, 3)
+        y_tile(0, 0, S, "u_raw1")
         evacuate(acc0a, 0, 0, HALF, bias[:, 0:1])
-        gather_words(1, HALF, S)
-        gather_words(2, HALF, S)
+        gather_words(2, HALF, S, "stage_u0")
         acc0b = product(0, HALF, S, 1, 3)
-        y_tile(0, HALF, S, "y0b")
         evacuate(acc0b, 0, HALF, S, bias[:, 0:1])
         u_q[1] = quantize(u_bf[1], P, "u1")
         clear(2, "stage_u1", nc.gpsimd)
@@ -239,8 +236,8 @@ def tile_list_tabhs_d_bias_kernel(tc, tab, w4_words, w4_scales, c, u, b, wgo, of
         scatter(0, HALF, S)
         store(0)
         u_q[2] = quantize(u_bf[2], P, "u2")
-        clear(3, "u0_codes", nc.gpsimd)
-        u_bf[3] = interleave(u_raw[3], P, "u_bf3", "u1_codes")
+        clear(3, "u1_codes", nc.gpsimd)
+        u_bf[3] = interleave(u_raw[3], P, "u_bf3", "u0_codes")
         scatter(1, 0, S)
         store(1)
         u_q[3] = quantize(u_bf[3], P, "u3")

@@ -23,8 +23,12 @@ P = 128
 PACK = 4
 PASSES = K // (P * PACK)
 ROW_TILES = M // P
-HALF = 128
-HALVES = S // HALF
+HALF = S // 2
+GROUP = 16
+QUADRANT = 32
+SCALE_ROWS = 4
+RUN = 4
+ALIGN = 64
 
 
 def tile_list_tabhs_d_bias_kernel(tc, tab, w4_words, w4_scales, c, u, b, wgo, offs, offs2, out):
@@ -33,220 +37,203 @@ def tile_list_tabhs_d_bias_kernel(tc, tab, w4_words, w4_scales, c, u, b, wgo, of
         keep = ctx.enter_context(tc.tile_pool(name="keep", bufs=1))
         psum = ctx.enter_context(tc.psum_pool(name="psum", bufs=1))
 
-        pick = keep.tile([P, S // 16], U16, name="pick")
-        place = keep.tile([P, S // 16], U16, name="place")
-        tab_planes = keep.tile([P, PASSES, T // 4], I32, name="tab_planes", align_bytes=64)
-        w_planes = keep.tile([P, PASSES, M // 4], I32, name="w_planes", align_bytes=64)
-        tab_words = {}
-        c_raw = keep.tile([P, PACK, S], F32, name="c_raw", tag="c_raw", align_bytes=64)
+        pick = keep.tile([P, S // GROUP], U16, name="pick")
+        place = keep.tile([P, S // GROUP], U16, name="place")
+        tab_planes = keep.tile([P, PASSES, T // 4], I32, name="tab_planes", align_bytes=ALIGN)
+        w_planes = keep.tile([P, PASSES, M // 4], I32, name="w_planes", align_bytes=ALIGN)
+        c_raw = keep.tile([P, PACK, S], F32, name="c_raw", tag="c_raw", align_bytes=ALIGN)
         weights = keep.tile([P, S], F32, name="weights")
         b_rows = keep.tile([P, P], F32, name="b_rows")
         ident = keep.tile([P, P], F32, name="ident")
-        placed = {}
-
-        def clear(m, tag, eng):
-            placed[m] = keep.tile([P, T], F32, name="placed%d" % m, tag=tag, align_bytes=64)
-            eng.memset(placed[m][:], 0.0)
 
         tab32 = tab.bitcast(I32)
-        w_scales32 = w4_scales.bitcast(I32)
-        u_rows = u.rearrange("(p j) n -> p j n", j=PACK)
-        w_rows = w4_words.bitcast(I32).rearrange("a p n -> p a n")
-        u_raw = {}
+        tab_words = {}
         w_words = {}
-
-        def load_table(lo, hi, eng):
-            tile = keep.tile([P, (hi - lo) * T], I32, name="tab_words%d" % lo, align_bytes=64)
-            rows = tab32[lo:hi, 0 : P * T].rearrange("a (p t) -> p a t", p=P)
-            eng.dma_start(tile[:].rearrange("p (a t) -> p a t", t=T), rows)
-            for a in range(lo, hi):
-                tab_words[a] = tile[:, (a - lo) * T : (a - lo + 1) * T]
-
-        def load_table_scales(engines):
-            first = P * T
-            rows = tab32[:, first : first + 4 * T].rearrange("a (q r t) -> r q a t", q=4, r=4)
-            for r in range(4):
-                engines[r].dma_start(tab_planes[r:P:32, :, :], rows[r])
-
-        def load_w_scales(eng, lo, hi):
-            rows = w_scales32.rearrange("a (q r) n -> r q a n", r=4)
-            for r in range(lo, hi):
-                eng.dma_start(w_planes[r:P:32, :, :], rows[r])
-
-        def load_u(lo, hi):
-            tile = keep.tile([P, PACK, (hi - lo) * P], F32, name="u_raw%d" % lo, tag="u_raw%d" % lo, align_bytes=64)
-            nc.sync.dma_start(tile[:], u_rows[:, :, lo * P : hi * P])
-            for m in range(lo, hi):
-                u_raw[m] = tile[:, :, (m - lo) * P : (m - lo + 1) * P]
-
-        def load_w(lo, hi):
-            tile = keep.tile([P, PASSES, (hi - lo) * 2 * P], U8, name="w_words%d" % lo, align_bytes=64)
-            nc.sync.dma_start(tile[:].bitcast(I32), w_rows[:, :, lo * P // 2 : hi * P // 2])
-            for m in range(lo, hi):
-                w_words[m] = [tile[:, a, (m - lo) * 2 * P : (m - lo + 1) * 2 * P] for a in range(PASSES)]
-
-        def interleave(raw, width, name, tag):
-            grouped = keep.tile([P, width, PACK], BF16, name=name, tag=tag, align_bytes=64)
-            nc.scalar.activation(
-                grouped[:].rearrange("p (w i) j -> p w j i", i=4),
-                raw.rearrange("p j (w i) -> p w j i", i=4),
-                COPY,
-            )
-            return grouped
-
-        def quantize(grouped, width, name):
-            codes = keep.tile([P, width], U32, name=name + "_codes", tag=name + "_codes", align_bytes=64)
-            scales = keep.tile([P, width], U8, name=name + "_scales", tag=name + "_scales", align_bytes=64)
-            nc.vector.quantize_mx(
-                out=codes[:].bitcast(FP8X4),
-                scales=scales[:],
-                in_=grouped[:].rearrange("p w j -> p (w j)"),
-            )
-            return codes, scales
-
-        c_codes = keep.tile([P, S], U32, name="c_codes", align_bytes=64)
-        c_scales = keep.tile([P, S], U8, name="c_scales", align_bytes=64)
-
-        def quantize_c(grouped, lo, hi):
-            nc.vector.quantize_mx(
-                out=c_codes[:, lo:hi].bitcast(FP8X4),
-                scales=c_scales[:, lo:hi],
-                in_=grouped[:].rearrange("p w j -> p (w j)"),
-            )
-
-        got_scales = [keep.tile([P, S], U8, name="got_scales%d" % a, align_bytes=64) for a in range(PASSES)]
-        got_words = {}
+        u_raw = {}
+        placed = {}
 
 
-        def gather_scales(a, lo, hi):
-            window = tab_planes[:, a, :].bitcast(U8)
-            nc.vector.tensor_copy(got_scales[a][:, lo:hi], window.indirect(pick[:, lo // 16 : hi // 16]))
+        def load_table(first, last):
+            tile = keep.tile([P, (last - first) * T], I32, name="tab_words%d" % first, align_bytes=ALIGN)
+            rows = tab32[first:last, 0 : P * T].rearrange("a (p t) -> p a t", p=P)
+            nc.sync.dma_start(tile[:].rearrange("p (a t) -> p a t", t=T), rows)
+            for a in range(first, last):
+                tab_words[a] = tile[:, (a - first) * T : (a - first + 1) * T]
 
-        def gather_words(a, lo, hi, tag):
-            tile = keep.tile([P, hi - lo], U32, name="got_words%d_%d" % (a, lo), tag=tag, align_bytes=64)
-            window = tab_words[a].bitcast(U32)
-            nc.vector.tensor_copy(tile[:], window.indirect(pick[:, lo // 16 : hi // 16]))
-            for x in range(lo, hi, HALF):
-                got_words[a, x] = tile[:, x - lo : x - lo + HALF]
+        def load_table_scales():
+            rows = tab32[:, P * T : P * T + SCALE_ROWS * T].rearrange("a (q r t) -> r q a t", q=4, r=SCALE_ROWS)
+            for r in range(SCALE_ROWS):
+                queue = nc.sync if r % 2 else nc.scalar
+                queue.dma_start(tab_planes[r:P:QUADRANT, :, :], rows[r])
 
-        u_q = {}
-        u_bf = {}
+        def load_w_scales(first, last):
+            rows = w4_scales.bitcast(I32).rearrange("a (q r) n -> r q a n", r=SCALE_ROWS)
+            for r in range(first, last):
+                nc.sync.dma_start(w_planes[r:P:QUADRANT, :, :], rows[r])
 
-        def table_pass(acc, m, a, lo, first, last, base):
-            nc.tensor.matmul_mx(
-                out=acc[:, lo - base : lo - base + HALF],
-                lhsT=w_words[m][a].bitcast(FP4X4),
-                lhsT_scale=w_planes[:, a, :].bitcast(U8)[:, P * m : P * (m + 1)],
-                rhs=got_words[a, lo].bitcast(FP8X4),
-                rhs_scale=got_scales[a][:, lo : lo + HALF],
-                start=first,
-                stop=last,
-            )
+        def load_u(m):
+            tile = keep.tile([P, PACK, P], F32, name="u_raw%d" % m, tag="u_raw%d" % m, align_bytes=ALIGN)
+            nc.sync.dma_start(tile[:], u.rearrange("(p i) n -> p i n", i=PACK)[:, :, m * P : (m + 1) * P])
+            u_raw[m] = tile[:]
 
-        def dense_pass(acc, m, lo, hi, first, last):
-            nc.tensor.matmul_mx(
-                out=acc[:],
-                lhsT=u_q[m][0][:].bitcast(FP8X4),
-                lhsT_scale=u_q[m][1][:],
-                rhs=c_codes[:, lo:hi].bitcast(FP8X4),
-                rhs_scale=c_scales[:, lo:hi],
-                start=first,
-                stop=last,
-            )
+        def load_w(first, last):
+            tile = keep.tile([P, PASSES, (last - first) * 2 * P], U8, name="w_words%d" % first, align_bytes=ALIGN)
+            rows = w4_words.bitcast(I32).rearrange("a p n -> p a n")
+            nc.sync.dma_start(tile[:].bitcast(I32), rows[:, :, first * P // 2 : last * P // 2])
+            for m in range(first, last):
+                w_words[m] = [tile[:, a, (m - first) * 2 * P : (m - first + 1) * 2 * P] for a in range(PASSES)]
 
-        def product(m, lo, hi, bank, dense_at):
-            acc = psum.tile([P, hi - lo], F32, name="acc%d_%d" % (m, lo), tag="bank%d" % bank)
-            steps = [(a, x) for a in range(PASSES) for x in range(lo, hi, HALF)]
-            steps.insert(dense_at * (hi - lo) // HALF, None)
-            for n, step in enumerate(steps):
-                if step is None:
-                    dense_pass(acc, m, lo, hi, n == 0, n == len(steps) - 1)
-                else:
-                    table_pass(acc, m, step[0], step[1], n == 0, n == len(steps) - 1, lo)
-            return acc
-
-        y = {}
-
-        def y_tile(m, lo, hi, tag):
-            tile = keep.tile([P, hi - lo], F32, name="y%d_%d" % (m, lo), tag=tag, align_bytes=64)
-            y[m, lo, hi] = tile[:]
-            for x in range(lo, hi, HALF):
-                y[m, x, x + HALF] = tile[:, x - lo : x - lo + HALF]
-
-        def evacuate(acc, m, lo, hi, column):
-            nc.scalar.activation(y[m, lo, hi], acc[:], IDENTITY, bias=column)
-
-        def scatter(m, lo, hi):
-            nc.vector.tensor_tensor(placed[m][:].indirect(place[:, lo // 16 : hi // 16]), y[m, lo, hi], weights[:, lo:hi], MULT)
-
-        def store(m):
-            nc.sync.dma_start(out[m * P : (m + 1) * P, :], placed[m][:])
+        def clear(m, tag, engine):
+            placed[m] = keep.tile([P, T], F32, name="placed%d" % m, tag=tag, align_bytes=ALIGN)
+            engine.memset(placed[m][:], 0.0)
 
         nc.gpsimd.memset(tab_planes[:], 0)
         nc.vector.memset(w_planes[:], 0)
-        load_table(0, 1, nc.sync)
+
+        load_table(0, 1)
         nc.sync.dma_start(pick[:], offs)
-        load_table_scales([nc.sync] * 4)
-        nc.sync.dma_start(c_raw[:], c.rearrange("(p j) s -> p j s", j=PACK))
-        load_table(1, 3, nc.sync)
-        load_w_scales(nc.sync, 0, 1)
-        load_u(0, 1)
+        load_table_scales()
+        nc.sync.dma_start(c_raw[:], c.rearrange("(p i) s -> p i s", i=PACK))
+        load_table(1, PASSES)
+        load_w_scales(0, 1)
+        load_u(0)
         load_w(0, 2)
-        load_w_scales(nc.sync, 1, 4)
-        load_u(1, 2)
+        load_w_scales(1, SCALE_ROWS)
+        load_u(1)
         nc.sync.dma_start(weights[:], wgo)
         nc.sync.dma_start(place[:], offs2)
-        load_u(2, 3)
-        load_w(2, 4)
-        load_u(3, 4)
+        load_u(2)
+        load_w(2, ROW_TILES)
+        load_u(3)
+
         nc.gpsimd.memset(b_rows[:], 0.0)
         nc.gpsimd.dma_start(b_rows[0:ROW_TILES, :], b.rearrange("(m p) -> m p", p=P))
         make_identity(nc, ident[:])
         clear(0, "placed0", nc.vector)
         clear(1, "placed1", nc.vector)
 
-        b_t = psum.tile([P, P], F32, name="b_t", tag="bank7")
+
+        def interleave(raw, width, name, tag):
+            grouped = keep.tile([P, width, PACK], BF16, name=name, tag=tag, align_bytes=ALIGN)
+            nc.scalar.activation(
+                grouped[:].rearrange("p (w x) i -> p w i x", x=RUN),
+                raw.rearrange("p i (w x) -> p w i x", x=RUN),
+                COPY,
+            )
+            return grouped
+
+        def quantize(grouped, width, name):
+            codes = keep.tile([P, width], U32, name=name + "_codes", tag=name + "_codes", align_bytes=ALIGN)
+            scales = keep.tile([P, width], U8, name=name + "_scales", align_bytes=ALIGN)
+            nc.vector.quantize_mx(
+                out=codes[:].bitcast(FP8X4),
+                scales=scales[:],
+                in_=grouped[:].rearrange("p w i -> p (w i)"),
+            )
+            return codes, scales
+
+        got_scales = {}
+        got_words = {}
+        u_q = {}
+        y = {}
+
+        def gather_scales(a):
+            got_scales[a] = keep.tile([P, S], U8, name="got_scales%d" % a, align_bytes=ALIGN)
+            nc.vector.tensor_copy(got_scales[a][:], tab_planes[:, a, :].bitcast(U8).indirect(pick[:]))
+
+        def gather_words(a, lo, hi, tag):
+            tile = keep.tile([P, hi - lo], U32, name="got_words%d_%d" % (a, lo), tag=tag, align_bytes=ALIGN)
+            nc.vector.tensor_copy(tile[:], tab_words[a].bitcast(U32).indirect(pick[:, lo // GROUP : hi // GROUP]))
+            for x in range(lo, hi, HALF):
+                got_words[a, x] = tile[:, x - lo : x - lo + HALF]
+
+        def product(m, lo, hi, bank):
+            acc = psum.tile([P, hi - lo], F32, name="acc%d_%d" % (m, lo), tag=bank)
+            for a in range(PASSES):
+                for x in range(lo, hi, HALF):
+                    nc.tensor.matmul_mx(
+                        out=acc[:, x - lo : x - lo + HALF],
+                        lhsT=w_words[m][a].bitcast(FP4X4),
+                        lhsT_scale=w_planes[:, a, :].bitcast(U8)[:, P * m : P * (m + 1)],
+                        rhs=got_words[a, x].bitcast(FP8X4),
+                        rhs_scale=got_scales[a][:, x : x + HALF],
+                        start=(a == 0 and x == lo),
+                        stop=False,
+                    )
+            nc.tensor.matmul_mx(
+                out=acc[:],
+                lhsT=u_q[m][0][:].bitcast(FP8X4),
+                lhsT_scale=u_q[m][1][:],
+                rhs=c_codes[:, lo:hi].bitcast(FP8X4),
+                rhs_scale=c_scales[:, lo:hi],
+                start=False,
+                stop=True,
+            )
+            return acc
+
+        def y_tile(m, tag):
+            tile = keep.tile([P, S], F32, name="y%d" % m, tag=tag, align_bytes=ALIGN)
+            y[m, 0, S] = tile[:]
+            y[m, 0, HALF] = tile[:, 0:HALF]
+            y[m, HALF, S] = tile[:, HALF:S]
+
+        def add_bias(acc, m, lo, hi):
+            nc.scalar.activation(y[m, lo, hi], acc[:], IDENTITY, bias=bias[:, m : m + 1])
+
+        def scatter(m, lo, hi):
+            window = placed[m][:].indirect(place[:, lo // GROUP : hi // GROUP])
+            nc.vector.tensor_tensor(window, y[m, lo, hi], weights[:, lo:hi], MULT)
+
+        def store(m):
+            nc.sync.dma_start(out[m * P : (m + 1) * P, :], placed[m][:])
+
+
+        b_t = psum.tile([P, P], F32, name="b_t", tag="bank_b")
         nc.tensor.transpose(b_t[:], b_rows[:], ident[:])
         c_bf = interleave(c_raw[:], S, "c_bf", "stage_c")
-        u_bf[0] = interleave(u_raw[0], P, "u_bf0", "stage_u0")
-        bias = keep.tile([P, ROW_TILES], F32, name="bias", tag="u_raw0", align_bytes=64)
+        u_bf0 = interleave(u_raw[0], P, "u_bf0", "stage_u0")
+        bias = keep.tile([P, ROW_TILES], F32, name="bias", tag="u_raw0", align_bytes=ALIGN)
         nc.scalar.activation(bias[:], b_t[:, 0:ROW_TILES], COPY)
-        u_bf[1] = interleave(u_raw[1], P, "u_bf1", "stage_u1")
+        u_bf1 = interleave(u_raw[1], P, "u_bf1", "stage_u1")
 
         gather_words(0, 0, S, "words0")
         for a in range(PASSES):
-            gather_scales(a, 0, S)
+            gather_scales(a)
         gather_words(1, 0, S, "words1")
         gather_words(2, 0, HALF, "words2")
-        quantize_c(c_bf, 0, S)
-        u_q[0] = quantize(u_bf[0], P, "u0")
-        acc0a = product(0, 0, HALF, 0, 3)
-        y_tile(0, 0, S, "u_raw1")
-        evacuate(acc0a, 0, 0, HALF, bias[:, 0:1])
+        c_codes, c_scales = quantize(c_bf, S, "c")
+        u_q[0] = quantize(u_bf0, P, "u0")
+
+        acc_first = product(0, 0, HALF, "bank_even")
+        y_tile(0, "u_raw1")
+        add_bias(acc_first, 0, 0, HALF)
         gather_words(2, HALF, S, "stage_u0")
-        acc0b = product(0, HALF, S, 1, 3)
-        evacuate(acc0b, 0, HALF, S, bias[:, 0:1])
-        u_q[1] = quantize(u_bf[1], P, "u1")
+        acc_second = product(0, HALF, S, "bank_odd")
+        add_bias(acc_second, 0, HALF, S)
+        u_q[1] = quantize(u_bf1, P, "u1")
+
         clear(2, "stage_u1", nc.gpsimd)
         scatter(0, 0, HALF)
-        u_bf[2] = interleave(u_raw[2], P, "u_bf2", "u0_codes")
-        acc1 = product(1, 0, S, 0, 3)
-        y_tile(1, 0, S, "u_raw2")
-        evacuate(acc1, 1, 0, S, bias[:, 1:2])
+        u_bf2 = interleave(u_raw[2], P, "u_bf2", "u0_codes")
+        acc1 = product(1, 0, S, "bank_even")
+        y_tile(1, "u_raw2")
+        add_bias(acc1, 1, 0, S)
         scatter(0, HALF, S)
         store(0)
-        u_q[2] = quantize(u_bf[2], P, "u2")
-        clear(3, "u1_codes", nc.gpsimd)
-        u_bf[3] = interleave(u_raw[3], P, "u_bf3", "u0_codes")
+
+        u_q[2] = quantize(u_bf2, P, "u2")
+        u_bf3 = interleave(u_raw[3], P, "u_bf3", "u0_codes")
         scatter(1, 0, S)
         store(1)
-        u_q[3] = quantize(u_bf[3], P, "u3")
-        acc2 = product(2, 0, S, 1, 3)
-        y_tile(2, 0, S, "u_raw3")
-        evacuate(acc2, 2, 0, S, bias[:, 2:3])
-        acc3 = product(3, 0, S, 0, 3)
-        y_tile(3, 0, S, "y3")
-        evacuate(acc3, 3, 0, S, bias[:, 3:4])
+
+        u_q[3] = quantize(u_bf3, P, "u3")
+        acc2 = product(2, 0, S, "bank_odd")
+        clear(3, "u2_codes", nc.gpsimd)
+        y_tile(2, "u_raw3")
+        add_bias(acc2, 2, 0, S)
+        acc3 = product(3, 0, S, "bank_even")
+        y_tile(3, "y3")
+        add_bias(acc3, 3, 0, S)
         scatter(2, 0, S)
         store(2)
         scatter(3, 0, S)

@@ -83,9 +83,9 @@ def tile_list_tabhs_d_bias_kernel(tc, tab, w4_words, w4_scales, c, u, b, wgo, of
             for m in range(first, last):
                 w_words[m] = [tile[:, a, (m - first) * 2 * P : (m - first + 1) * 2 * P] for a in range(PASSES)]
 
-        def clear(m, tag, engine):
-            placed[m] = keep.tile([P, T], F32, name="placed%d" % m, tag=tag, align_bytes=ALIGN)
-            engine.memset(placed[m][:], 0.0)
+        def clear(m):
+            placed[m] = keep.tile([P, T], F32, name="placed%d" % m, align_bytes=ALIGN)
+            nc.vector.memset(placed[m][:], 0.0)
 
         nc.gpsimd.memset(tab_planes[:], 0)
         nc.vector.memset(w_planes[:], 0)
@@ -109,8 +109,8 @@ def tile_list_tabhs_d_bias_kernel(tc, tab, w4_words, w4_scales, c, u, b, wgo, of
         nc.gpsimd.memset(b_rows[:], 0.0)
         nc.gpsimd.dma_start(b_rows[0:ROW_TILES, :], b.rearrange("(m p) -> m p", p=P))
         make_identity(nc, ident[:])
-        clear(0, "placed0", nc.vector)
-        clear(1, "placed1", nc.vector)
+        for m in range(ROW_TILES):
+            clear(m)
 
 
         def interleave(raw, width, name, tag):
@@ -212,7 +212,6 @@ def tile_list_tabhs_d_bias_kernel(tc, tab, w4_words, w4_scales, c, u, b, wgo, of
         add_bias(acc_second, 0, HALF, S)
         u_q[1] = quantize(u_bf1, P, "u1")
 
-        clear(2, "stage_u1", nc.gpsimd)
         scatter(0, 0, HALF)
         u_bf2 = interleave(u_raw[2], P, "u_bf2", "u0_codes")
         acc1 = product(1, 0, S, "bank_even")
@@ -228,7 +227,6 @@ def tile_list_tabhs_d_bias_kernel(tc, tab, w4_words, w4_scales, c, u, b, wgo, of
 
         u_q[3] = quantize(u_bf3, P, "u3")
         acc2 = product(2, 0, S, "bank_odd")
-        clear(3, "u2_codes", nc.gpsimd)
         y_tile(2, "u_raw3")
         add_bias(acc2, 2, 0, S)
         acc3 = product(3, 0, S, "bank_even")

@@ -40,7 +40,7 @@ def tile_list_tabhs_d_bias_kernel(tc, tab, w4_words, w4_scales, c, u, b, wgo, of
         pick = keep.tile([P, S // GROUP], U16, name="pick")
         place = keep.tile([P, S // GROUP], U16, name="place")
         tab_planes = keep.tile([P, PASSES, T // 4], I32, name="tab_planes", align_bytes=ALIGN)
-        w_planes = keep.tile([P, PASSES, M // 4], I32, name="w_planes", align_bytes=ALIGN)
+        w_planes = [keep.tile([P, PASSES, M // 8], I32, name="w_planes%d" % h, align_bytes=ALIGN) for h in range(2)]
         c_raw = keep.tile([P, PACK, S], F32, name="c_raw", tag="c_raw", align_bytes=ALIGN)
         weights = keep.tile([P, S], F32, name="weights")
         b_rows = keep.tile([P, P], F32, name="b_rows")
@@ -66,10 +66,10 @@ def tile_list_tabhs_d_bias_kernel(tc, tab, w4_words, w4_scales, c, u, b, wgo, of
                 queue = nc.sync if r % 2 else nc.scalar
                 queue.dma_start(tab_planes[r:P:QUADRANT, :, :], rows[r])
 
-        def load_w_scales(first, last):
+        def load_w_scales(h, first, last):
             rows = w4_scales.bitcast(I32).rearrange("a (q r) n -> r q a n", r=SCALE_ROWS)
             for r in range(first, last):
-                nc.sync.dma_start(w_planes[r:P:QUADRANT, :, :], rows[r])
+                nc.sync.dma_start(w_planes[h][r:P:QUADRANT, :, :], rows[r][:, :, h * M // 8 : (h + 1) * M // 8])
 
         def load_u(m):
             tile = keep.tile([P, PACK, P], F32, name="u_raw%d" % m, tag="u_raw%d" % m, align_bytes=ALIGN)
@@ -88,22 +88,24 @@ def tile_list_tabhs_d_bias_kernel(tc, tab, w4_words, w4_scales, c, u, b, wgo, of
             nc.vector.memset(placed[m][:], 0.0)
 
         nc.gpsimd.memset(tab_planes[:], 0)
-        nc.vector.memset(w_planes[:], 0)
+        for planes in w_planes:
+            nc.vector.memset(planes[:], 0)
 
         load_table(0, 1)
         nc.sync.dma_start(pick[:], offs)
         load_table_scales()
         nc.sync.dma_start(c_raw[:], c.rearrange("(p i) s -> p i s", i=PACK))
         load_table(1, PASSES)
-        load_w_scales(0, 1)
+        load_w_scales(0, 0, 1)
         load_u(0)
         load_w(0, 2)
-        load_w_scales(1, SCALE_ROWS)
+        load_w_scales(0, 1, SCALE_ROWS)
         load_u(1)
         nc.sync.dma_start(weights[:], wgo)
         nc.sync.dma_start(place[:], offs2)
         load_u(2)
         load_w(2, ROW_TILES)
+        load_w_scales(1, 0, SCALE_ROWS)
         load_u(3)
 
         nc.gpsimd.memset(b_rows[:], 0.0)
@@ -154,7 +156,7 @@ def tile_list_tabhs_d_bias_kernel(tc, tab, w4_words, w4_scales, c, u, b, wgo, of
                     nc.tensor.matmul_mx(
                         out=acc[:, x - lo : x - lo + HALF],
                         lhsT=w_words[m][a].bitcast(FP4X4),
-                        lhsT_scale=w_planes[:, a, :].bitcast(U8)[:, P * m : P * (m + 1)],
+                        lhsT_scale=w_planes[m // 2][:, a, :].bitcast(U8)[:, P * (m % 2) : P * (m % 2 + 1)],
                         rhs=got_words[a, x].bitcast(FP8X4),
                         rhs_scale=got_scales[a][:, x : x + HALF],
                         start=(a == 0 and x == lo),

@@ -23,6 +23,7 @@ P = 128
 PACK = 4
 PASSES = K // (P * PACK)
 ROW_TILES = M // P
+EARLY_TILES = 2
 HALF = S // 2
 GROUP = 16
 QUADRANT = 32
@@ -40,7 +41,6 @@ def tile_list_tabhs_d_bias_kernel(tc, tab, w4_words, w4_scales, c, u, b, wgo, of
         pick = keep.tile([P, S // GROUP], U16, name="pick")
         place = keep.tile([P, S // GROUP], U16, name="place")
         tab_planes = keep.tile([P, PASSES, T // 4], I32, name="tab_planes", align_bytes=ALIGN)
-        w_planes = [keep.tile([P, PASSES, M // 8], I32, name="w_planes%d" % h, align_bytes=ALIGN) for h in range(2)]
         c_raw = keep.tile([P, PACK, S], F32, name="c_raw", tag="c_raw", align_bytes=ALIGN)
         weights = keep.tile([P, S], F32, name="weights")
         b_rows = keep.tile([P, P], F32, name="b_rows")
@@ -48,6 +48,7 @@ def tile_list_tabhs_d_bias_kernel(tc, tab, w4_words, w4_scales, c, u, b, wgo, of
 
         tab32 = tab.bitcast(I32)
         tab_words = {}
+        w_planes = {}
         w_words = {}
         u_raw = {}
         placed = {}
@@ -66,10 +67,19 @@ def tile_list_tabhs_d_bias_kernel(tc, tab, w4_words, w4_scales, c, u, b, wgo, of
                 queue = nc.sync if r % 2 else nc.scalar
                 queue.dma_start(tab_planes[r:P:QUADRANT, :, :], rows[r])
 
-        def load_w_scales(h, first, last):
+        def clear_w_planes(first, last):
+            tile = keep.tile([P, PASSES, (last - first) * P // 4], I32, name="w_planes%d" % first, align_bytes=ALIGN)
+            nc.vector.memset(tile[:], 0)
+            for m in range(first, last):
+                columns = slice((m - first) * P, (m - first + 1) * P)
+                w_planes[m] = [tile[:, a, :].bitcast(U8)[:, columns] for a in range(PASSES)]
+            return tile
+
+        def load_w_scales(tile, first_tile, first, last):
             rows = w4_scales.bitcast(I32).rearrange("a (q r) n -> r q a n", r=SCALE_ROWS)
+            start = first_tile * P // 4
             for r in range(first, last):
-                nc.sync.dma_start(w_planes[h][r:P:QUADRANT, :, :], rows[r][:, :, h * M // 8 : (h + 1) * M // 8])
+                nc.sync.dma_start(tile[r:P:QUADRANT, :, :], rows[r][:, :, start : start + tile.shape[2]])
 
         def load_u(m):
             tile = keep.tile([P, PACK, P], F32, name="u_raw%d" % m, tag="u_raw%d" % m, align_bytes=ALIGN)
@@ -88,25 +98,26 @@ def tile_list_tabhs_d_bias_kernel(tc, tab, w4_words, w4_scales, c, u, b, wgo, of
             nc.vector.memset(placed[m][:], 0.0)
 
         nc.gpsimd.memset(tab_planes[:], 0)
-        for planes in w_planes:
-            nc.vector.memset(planes[:], 0)
+        early_planes = clear_w_planes(0, EARLY_TILES)
+        late_planes = {m: clear_w_planes(m, m + 1) for m in range(EARLY_TILES, ROW_TILES)}
 
         load_table(0, 1)
         nc.sync.dma_start(pick[:], offs)
         load_table_scales()
         nc.sync.dma_start(c_raw[:], c.rearrange("(p i) s -> p i s", i=PACK))
         load_table(1, PASSES)
-        load_w_scales(0, 0, 1)
+        load_w_scales(early_planes, 0, 0, 1)
         load_u(0)
-        load_w(0, 2)
-        load_w_scales(0, 1, SCALE_ROWS)
+        load_w(0, EARLY_TILES)
+        load_w_scales(early_planes, 0, 1, SCALE_ROWS)
         load_u(1)
         nc.sync.dma_start(weights[:], wgo)
         nc.sync.dma_start(place[:], offs2)
         load_u(2)
-        load_w(2, ROW_TILES)
-        load_w_scales(1, 0, SCALE_ROWS)
+        load_w(EARLY_TILES, ROW_TILES)
         load_u(3)
+        for m in range(EARLY_TILES, ROW_TILES):
+            load_w_scales(late_planes[m], m, 0, SCALE_ROWS)
 
         nc.gpsimd.memset(b_rows[:], 0.0)
         nc.gpsimd.dma_start(b_rows[0:ROW_TILES, :], b.rearrange("(m p) -> m p", p=P))
@@ -156,7 +167,7 @@ def tile_list_tabhs_d_bias_kernel(tc, tab, w4_words, w4_scales, c, u, b, wgo, of
                     nc.tensor.matmul_mx(
                         out=acc[:, x - lo : x - lo + HALF],
                         lhsT=w_words[m][a].bitcast(FP4X4),
-                        lhsT_scale=w_planes[m // 2][:, a, :].bitcast(U8)[:, P * (m % 2) : P * (m % 2 + 1)],
+                        lhsT_scale=w_planes[m][a],
                         rhs=got_words[a, x].bitcast(FP8X4),
                         rhs_scale=got_scales[a][:, x : x + HALF],
                         start=(a == 0 and x == lo),

@@ -157,22 +157,22 @@ def tile_list_tabhs_d_bias_kernel(tc, tab, w4_words, w4_scales, c, u, b, wgo, of
         def gather_words(a, lo, hi, tag):
             tile = keep.tile([P, hi - lo], U32, name="got_words%d_%d" % (a, lo), tag=tag, align_bytes=ALIGN)
             nc.vector.tensor_copy(tile[:], tab_words[a].bitcast(U32).indirect(pick[:, lo // GROUP : hi // GROUP]))
+            got_words[a, lo, hi] = tile[:]
             for x in range(lo, hi, HALF):
-                got_words[a, x] = tile[:, x - lo : x - lo + HALF]
+                got_words[a, x, x + HALF] = tile[:, x - lo : x - lo + HALF]
 
-        def product(m, lo, hi, bank):
+        def product(m, lo, hi, bank, order):
             acc = psum.tile([P, hi - lo], F32, name="acc%d_%d" % (m, lo), tag=bank)
-            for a in range(PASSES):
-                for x in range(lo, hi, HALF):
-                    nc.tensor.matmul_mx(
-                        out=acc[:, x - lo : x - lo + HALF],
-                        lhsT=w_words[m][a].bitcast(FP4X4),
-                        lhsT_scale=w_planes[m][a],
-                        rhs=got_words[a, x].bitcast(FP8X4),
-                        rhs_scale=got_scales[a][:, x : x + HALF],
-                        start=(a == 0 and x == lo),
-                        stop=False,
-                    )
+            for i, (a, x, end) in enumerate(order):
+                nc.tensor.matmul_mx(
+                    out=acc[:, x - lo : end - lo],
+                    lhsT=w_words[m][a].bitcast(FP4X4),
+                    lhsT_scale=w_planes[m][a],
+                    rhs=got_words[a, x, end].bitcast(FP8X4),
+                    rhs_scale=got_scales[a][:, x:end],
+                    start=(i == 0),
+                    stop=False,
+                )
             nc.tensor.matmul_mx(
                 out=acc[:],
                 lhsT=u_q[m][0][:].bitcast(FP8X4),
@@ -217,17 +217,18 @@ def tile_list_tabhs_d_bias_kernel(tc, tab, w4_words, w4_scales, c, u, b, wgo, of
         c_codes, c_scales = quantize(c_bf, S, "c")
         u_q[0] = quantize(u_bf0, P, "u0")
 
-        acc_first = product(0, 0, HALF, "bank_even")
+        acc_first = product(0, 0, HALF, "bank_first", [(a, 0, HALF) for a in range(PASSES)])
         y_tile(0, "u_raw1")
         add_bias(acc_first, 0, 0, HALF)
         gather_words(2, HALF, S, "stage_u0")
-        acc_second = product(0, HALF, S, "bank_odd")
+        acc_second = product(0, HALF, S, "bank_even", [(a, HALF, S) for a in range(PASSES)])
         add_bias(acc_second, 0, HALF, S)
         u_q[1] = quantize(u_bf1, P, "u1")
 
         scatter(0, 0, HALF)
         u_bf2 = interleave(u_raw[2], P, "u_bf2", "u0_codes")
-        acc1 = product(1, 0, S, "bank_even")
+        whole = [(2, HALF, S), (2, 0, HALF), (0, 0, S), (1, 0, S)]
+        acc1 = product(1, 0, S, "bank_odd", whole)
         y_tile(1, "u_raw2")
         add_bias(acc1, 1, 0, S)
         scatter(0, HALF, S)
@@ -239,10 +240,10 @@ def tile_list_tabhs_d_bias_kernel(tc, tab, w4_words, w4_scales, c, u, b, wgo, of
         store(1)
 
         u_q[3] = quantize(u_bf3, P, "u3")
-        acc2 = product(2, 0, S, "bank_odd")
+        acc2 = product(2, 0, S, "bank_even", whole)
         y_tile(2, "u_raw3")
         add_bias(acc2, 2, 0, S)
-        acc3 = product(3, 0, S, "bank_even")
+        acc3 = product(3, 0, S, "bank_odd", whole)
         y_tile(3, "y3")
         add_bias(acc3, 3, 0, S)
         scatter(2, 0, S)

@@ -18,6 +18,7 @@ FP4X4 = mybir.dt.float4_e2m1fn_x4
 IDENTITY = mybir.ActivationFunctionType.Identity
 COPY = mybir.ActivationFunctionType.Copy
 MULT = mybir.AluOpType.mult
+ADD = mybir.AluOpType.add
 
 P = 128
 PACK = 4
@@ -218,14 +219,17 @@ def tile_list_tabhs_d_bias_kernel(tc, tab, w4_words, w4_scales, c, u, b, wgo, of
         u_q[0] = quantize(u_bf0, P, "u0")
 
         acc_first = product(0, 0, HALF, "bank_first", [(a, 0, HALF) for a in range(PASSES)])
-        y_tile(0, "u_raw1")
-        add_bias(acc_first, 0, 0, HALF)
         gather_words(2, HALF, S, "stage_u0")
+        y_first = keep.tile([P, HALF], F32, name="y_first", align_bytes=ALIGN)
+        y[0, 0, HALF] = y_first[:]
+        nc.vector.tensor_scalar(y_first[:], acc_first[:], bias[:, 0:1], None, ADD)
+        y_second = keep.tile([P, HALF], F32, name="y_second", tag="u_raw1", align_bytes=ALIGN)
+        y[0, HALF, S] = y_second[:]
         acc_second = product(0, HALF, S, "bank_even", [(a, HALF, S) for a in range(PASSES)])
         add_bias(acc_second, 0, HALF, S)
-        u_q[1] = quantize(u_bf1, P, "u1")
 
         scatter(0, 0, HALF)
+        u_q[1] = quantize(u_bf1, P, "u1")
         u_bf2 = interleave(u_raw[2], P, "u_bf2", "u0_codes")
         whole = [(2, HALF, S), (2, 0, HALF), (0, 0, S), (1, 0, S)]
         acc1 = product(1, 0, S, "bank_odd", whole)

@@ -18,7 +18,6 @@ FP4X4 = mybir.dt.float4_e2m1fn_x4
 IDENTITY = mybir.ActivationFunctionType.Identity
 COPY = mybir.ActivationFunctionType.Copy
 MULT = mybir.AluOpType.mult
-ADD = mybir.AluOpType.add
 
 P = 128
 PACK = 4
@@ -37,6 +36,7 @@ def tile_list_tabhs_d_bias_kernel(tc, tab, w4_words, w4_scales, c, u, b, wgo, of
     nc = tc.nc
     with ExitStack() as ctx:
         keep = ctx.enter_context(tc.tile_pool(name="keep", bufs=1))
+        stage = ctx.enter_context(tc.tile_pool(name="stage", bufs=1))
         psum = ctx.enter_context(tc.psum_pool(name="psum", bufs=1))
 
         pick = keep.tile([P, S // GROUP], U16, name="pick")
@@ -127,14 +127,15 @@ def tile_list_tabhs_d_bias_kernel(tc, tab, w4_words, w4_scales, c, u, b, wgo, of
             clear(m)
 
 
-        def interleave(raw, width, name, tag):
-            grouped = keep.tile([P, width, PACK], BF16, name=name, tag=tag, align_bytes=ALIGN)
-            nc.scalar.activation(
-                grouped[:].rearrange("p (w x) i -> p w i x", x=RUN),
-                raw.rearrange("p i (w x) -> p w i x", x=RUN),
-                COPY,
-            )
+        def scalar_cast(out_view, in_view):
+            nc.scalar.activation(out_view, in_view, COPY)
+
+        def interleave(raw, grouped, cast=scalar_cast):
+            cast(grouped[:].rearrange("p (w x) i -> p w i x", x=RUN), raw.rearrange("p i (w x) -> p w i x", x=RUN))
             return grouped
+
+        def grouped_tile(width, name, tag):
+            return keep.tile([P, width, PACK], BF16, name=name, tag=tag, align_bytes=ALIGN)
 
         def quantize(grouped, width, name):
             codes = keep.tile([P, width], U32, name=name + "_codes", tag=name + "_codes", align_bytes=ALIGN)
@@ -155,8 +156,9 @@ def tile_list_tabhs_d_bias_kernel(tc, tab, w4_words, w4_scales, c, u, b, wgo, of
             got_scales[a] = keep.tile([P, S], U8, name="got_scales%d" % a, align_bytes=ALIGN)
             nc.vector.tensor_copy(got_scales[a][:], tab_planes[:, a, :].bitcast(U8).indirect(pick[:]))
 
-        def gather_words(a, lo, hi, tag):
-            tile = keep.tile([P, hi - lo], U32, name="got_words%d_%d" % (a, lo), tag=tag, align_bytes=ALIGN)
+        def gather_words(a, lo, hi, tile=None):
+            if tile is None:
+                tile = keep.tile([P, hi - lo], U32, name="got_words%d_%d" % (a, lo), align_bytes=ALIGN)
             nc.vector.tensor_copy(tile[:], tab_words[a].bitcast(U32).indirect(pick[:, lo // GROUP : hi // GROUP]))
             got_words[a, lo, hi] = tile[:]
             for x in range(lo, hi, HALF):
@@ -204,33 +206,35 @@ def tile_list_tabhs_d_bias_kernel(tc, tab, w4_words, w4_scales, c, u, b, wgo, of
 
         b_t = psum.tile([P, P], F32, name="b_t", tag="bank_b")
         nc.tensor.transpose(b_t[:], b_rows[:], ident[:])
-        c_bf = interleave(c_raw[:], S, "c_bf", "stage_c")
-        u_bf0 = interleave(u_raw[0], P, "u_bf0", "stage_u0")
+        c_bf = interleave(c_raw[:], grouped_tile(S, "c_bf", "c_bf"))
+        u_bf0 = interleave(u_raw[0], stage.tile([P, P, PACK], BF16, name="u_bf0", offset=0, align_bytes=ALIGN))
         bias = keep.tile([P, ROW_TILES], F32, name="bias", tag="u_raw0", align_bytes=ALIGN)
         nc.scalar.activation(bias[:], b_t[:, 0:ROW_TILES], COPY)
-        u_bf1 = interleave(u_raw[1], P, "u_bf1", "stage_u1")
 
-        gather_words(0, 0, S, "words0")
+        gather_words(0, 0, S)
         for a in range(PASSES):
             gather_scales(a)
-        gather_words(1, 0, S, "words1")
-        gather_words(2, 0, HALF, "words2")
+        gather_words(1, 0, S)
+        gather_words(2, 0, HALF)
         c_codes, c_scales = quantize(c_bf, S, "c")
         u_q[0] = quantize(u_bf0, P, "u0")
 
         acc_first = product(0, 0, HALF, "bank_first", [(a, 0, HALF) for a in range(PASSES)])
-        gather_words(2, HALF, S, "stage_u0")
+        gather_words(2, HALF, S, stage.tile([P, HALF], U32, name="got_last", offset=0, align_bytes=ALIGN))
         y_first = keep.tile([P, HALF], F32, name="y_first", align_bytes=ALIGN)
         y[0, 0, HALF] = y_first[:]
-        nc.vector.tensor_scalar(y_first[:], acc_first[:], bias[:, 0:1], None, ADD)
-        y_second = keep.tile([P, HALF], F32, name="y_second", tag="u_raw1", align_bytes=ALIGN)
+        add_bias(acc_first, 0, 0, HALF)
+        u_bf1 = interleave(
+            u_raw[1], stage.tile([P, P, PACK], BF16, name="u_bf1", offset=4 * HALF, align_bytes=ALIGN), nc.vector.tensor_copy
+        )
+        y_second = keep.tile([P, HALF], F32, name="y_second", align_bytes=ALIGN)
         y[0, HALF, S] = y_second[:]
         acc_second = product(0, HALF, S, "bank_even", [(a, HALF, S) for a in range(PASSES)])
         add_bias(acc_second, 0, HALF, S)
 
         scatter(0, 0, HALF)
         u_q[1] = quantize(u_bf1, P, "u1")
-        u_bf2 = interleave(u_raw[2], P, "u_bf2", "u0_codes")
+        u_bf2 = interleave(u_raw[2], grouped_tile(P, "u_bf2", "u0_codes"))
         whole = [(2, HALF, S), (2, 0, HALF), (0, 0, S), (1, 0, S)]
         acc1 = product(1, 0, S, "bank_odd", whole)
         y_tile(1, "u_raw2")
@@ -239,7 +243,7 @@ def tile_list_tabhs_d_bias_kernel(tc, tab, w4_words, w4_scales, c, u, b, wgo, of
         store(0)
 
         u_q[2] = quantize(u_bf2, P, "u2")
-        u_bf3 = interleave(u_raw[3], P, "u_bf3", "u0_codes")
+        u_bf3 = interleave(u_raw[3], grouped_tile(P, "u_bf3", "u0_codes"))
         scatter(1, 0, S)
         store(1)
 

@@ -22,6 +22,7 @@ MULT = mybir.AluOpType.mult
 P = 128
 PACK = 4
 PASSES = K // (P * PACK)
+DENSE = PASSES
 ROW_TILES = M // P
 EARLY_TILES = 2
 HALF = S // 2
@@ -36,7 +37,6 @@ def tile_list_tabhs_d_bias_kernel(tc, tab, w4_words, w4_scales, c, u, b, wgo, of
     nc = tc.nc
     with ExitStack() as ctx:
         keep = ctx.enter_context(tc.tile_pool(name="keep", bufs=1))
-        stage = ctx.enter_context(tc.tile_pool(name="stage", bufs=1))
         psum = ctx.enter_context(tc.psum_pool(name="psum", bufs=1))
 
         pick = keep.tile([P, S // GROUP], U16, name="pick")
@@ -167,24 +167,21 @@ def tile_list_tabhs_d_bias_kernel(tc, tab, w4_words, w4_scales, c, u, b, wgo, of
         def product(m, lo, hi, bank, order):
             acc = psum.tile([P, hi - lo], F32, name="acc%d_%d" % (m, lo), tag=bank)
             for i, (a, x, end) in enumerate(order):
+                if a == DENSE:
+                    lhs = u_q[m][0][:].bitcast(FP8X4), u_q[m][1][:]
+                    rhs = c_codes[:, x:end], c_scales[:, x:end]
+                else:
+                    lhs = w_words[m][a].bitcast(FP4X4), w_planes[m][a]
+                    rhs = got_words[a, x, end], got_scales[a][:, x:end]
                 nc.tensor.matmul_mx(
                     out=acc[:, x - lo : end - lo],
-                    lhsT=w_words[m][a].bitcast(FP4X4),
-                    lhsT_scale=w_planes[m][a],
-                    rhs=got_words[a, x, end].bitcast(FP8X4),
-                    rhs_scale=got_scales[a][:, x:end],
+                    lhsT=lhs[0],
+                    lhsT_scale=lhs[1],
+                    rhs=rhs[0].bitcast(FP8X4),
+                    rhs_scale=rhs[1],
                     start=(i == 0),
-                    stop=False,
+                    stop=(i == len(order) - 1),
                 )
-            nc.tensor.matmul_mx(
-                out=acc[:],
-                lhsT=u_q[m][0][:].bitcast(FP8X4),
-                lhsT_scale=u_q[m][1][:],
-                rhs=c_codes[:, lo:hi].bitcast(FP8X4),
-                rhs_scale=c_scales[:, lo:hi],
-                start=False,
-                stop=True,
-            )
             return acc
 
         def y_tile(m, tag):
@@ -207,8 +204,8 @@ def tile_list_tabhs_d_bias_kernel(tc, tab, w4_words, w4_scales, c, u, b, wgo, of
         b_t = psum.tile([P, P], F32, name="b_t", tag="bank_b")
         nc.tensor.transpose(b_t[:], b_rows[:], ident[:])
         c_bf = interleave(c_raw[:], grouped_tile(S, "c_bf", "c_bf"))
-        u_bf0 = interleave(u_raw[0], stage.tile([P, P, PACK], BF16, name="u_bf0", offset=0, align_bytes=ALIGN))
-        bias = keep.tile([P, ROW_TILES], F32, name="bias", tag="u_raw0", align_bytes=ALIGN)
+        u_bf0 = interleave(u_raw[0], grouped_tile(P, "u_bf0", "u_bf0"))
+        bias = keep.tile([P, ROW_TILES], F32, name="bias", align_bytes=ALIGN)
         nc.scalar.activation(bias[:], b_t[:, 0:ROW_TILES], COPY)
 
         gather_words(0, 0, S)
@@ -219,23 +216,22 @@ def tile_list_tabhs_d_bias_kernel(tc, tab, w4_words, w4_scales, c, u, b, wgo, of
         c_codes, c_scales = quantize(c_bf, S, "c")
         u_q[0] = quantize(u_bf0, P, "u0")
 
-        acc_first = product(0, 0, HALF, "bank_first", [(a, 0, HALF) for a in range(PASSES)])
-        gather_words(2, HALF, S, stage.tile([P, HALF], U32, name="got_last", offset=0, align_bytes=ALIGN))
+        acc_first = product(0, 0, HALF, "bank_first", [(a, 0, HALF) for a in (0, 1, 2, DENSE)])
+
         y_first = keep.tile([P, HALF], F32, name="y_first", align_bytes=ALIGN)
         y[0, 0, HALF] = y_first[:]
         add_bias(acc_first, 0, 0, HALF)
-        u_bf1 = interleave(
-            u_raw[1], stage.tile([P, P, PACK], BF16, name="u_bf1", offset=4 * HALF, align_bytes=ALIGN), nc.vector.tensor_copy
-        )
+        gather_words(2, HALF, S, keep.tile([P, HALF], U32, name="got_last", tag="u_raw0", align_bytes=ALIGN))
+        u_bf1 = interleave(u_raw[1], grouped_tile(P, "u_bf1", "u_bf1"), nc.vector.tensor_copy)
         y_second = keep.tile([P, HALF], F32, name="y_second", align_bytes=ALIGN)
         y[0, HALF, S] = y_second[:]
-        acc_second = product(0, HALF, S, "bank_even", [(a, HALF, S) for a in range(PASSES)])
+        acc_second = product(0, HALF, S, "bank_even", [(a, HALF, S) for a in (0, 1, DENSE, 2)])
         add_bias(acc_second, 0, HALF, S)
 
         scatter(0, 0, HALF)
         u_q[1] = quantize(u_bf1, P, "u1")
         u_bf2 = interleave(u_raw[2], grouped_tile(P, "u_bf2", "u0_codes"))
-        whole = [(2, HALF, S), (2, 0, HALF), (0, 0, S), (1, 0, S)]
+        whole = [(2, HALF, S), (2, 0, HALF), (0, 0, S), (1, 0, S), (DENSE, 0, S)]
         acc1 = product(1, 0, S, "bank_odd", whole)
         y_tile(1, "u_raw2")
         add_bias(acc1, 1, 0, S)

@@ -107,10 +107,10 @@ def tile_list_tabhs_d_bias_kernel(tc, tab, w4_words, w4_scales, c, u, b, wgo, of
         load_table_scales()
         nc.sync.dma_start(c_raw[:], c.rearrange("(p i) s -> p i s", i=PACK))
         load_table(1, PASSES)
-        load_w_scales(early_planes, 0, 0, 1)
+        load_w_scales(early_planes, 0, 0, 2)
         load_u(0)
         load_w(0, EARLY_TILES)
-        load_w_scales(early_planes, 0, 1, SCALE_ROWS)
+        load_w_scales(early_planes, 0, 2, SCALE_ROWS)
         load_u(1)
         nc.sync.dma_start(weights[:], wgo)
         nc.sync.dma_start(place[:], offs2)
@@ -230,7 +230,7 @@ def tile_list_tabhs_d_bias_kernel(tc, tab, w4_words, w4_scales, c, u, b, wgo, of
 
         scatter(0, 0, HALF)
         u_q[1] = quantize(u_bf1, P, "u1")
-        u_bf2 = interleave(u_raw[2], grouped_tile(P, "u_bf2", "u0_codes"))
+        u_bf2 = interleave(u_raw[2], grouped_tile(P, "u_bf2", "u_bf2"))
         whole = [(2, HALF, S), (2, 0, HALF), (0, 0, S), (1, 0, S), (DENSE, 0, S)]
         acc1 = product(1, 0, S, "bank_odd", whole)
         y_tile(1, "u_raw2")

@@ -116,9 +116,9 @@ def tile_list_tabhs_d_bias_kernel(tc, tab, w4_words, w4_scales, c, u, b, wgo, of
         nc.sync.dma_start(place[:], offs2)
         load_u(2)
         load_w(EARLY_TILES, ROW_TILES)
+        load_w_scales(late_planes[2], 2, 0, SCALE_ROWS)
         load_u(3)
-        for m in range(EARLY_TILES, ROW_TILES):
-            load_w_scales(late_planes[m], m, 0, SCALE_ROWS)
+        load_w_scales(late_planes[3], 3, 0, SCALE_ROWS)
 
         nc.gpsimd.memset(b_rows[:], 0.0)
         nc.gpsimd.dma_start(b_rows[0:ROW_TILES, :], b.rearrange("(m p) -> m p", p=P))

from contextlib import ExitStack

import concourse.mybir as mybir
from concourse.masks import make_identity

K, M, T, S = 1536, 512, 512, 256
L = 512
FLOPS = 2 * (K + L) * M * S

F32 = mybir.dt.float32
BF16 = mybir.dt.bfloat16
I32 = mybir.dt.int32
U32 = mybir.dt.uint32
U16 = mybir.dt.uint16
U8 = mybir.dt.uint8
FP8X4 = mybir.dt.float8_e4m3fn_x4
FP4X4 = mybir.dt.float4_e2m1fn_x4
IDENTITY = mybir.ActivationFunctionType.Identity
COPY = mybir.ActivationFunctionType.Copy
MULT = mybir.AluOpType.mult

P = 128
PACK = 4
PASSES = K // (P * PACK)
DENSE = PASSES
ROW_TILES = M // P
EARLY_TILES = 2
HALF = S // 2
GROUP = 16
QUADRANT = 32
SCALE_ROWS = 4
RUN = 4
ALIGN = 64


def tile_list_tabhs_d_bias_kernel(tc, tab, w4_words, w4_scales, c, u, b, wgo, offs, offs2, out):
    nc = tc.nc
    with ExitStack() as ctx:
        keep = ctx.enter_context(tc.tile_pool(name="keep", bufs=1))
        psum = ctx.enter_context(tc.psum_pool(name="psum", bufs=1))

        pick = keep.tile([P, S // GROUP], U16, name="pick")
        place = keep.tile([P, S // GROUP], U16, name="place")
        tab_planes = keep.tile([P, PASSES, T // 4], I32, name="tab_planes", align_bytes=ALIGN)
        c_raw = keep.tile([P, PACK, S], F32, name="c_raw", tag="c_raw", align_bytes=ALIGN)
        weights = keep.tile([P, S], F32, name="weights")
        b_rows = keep.tile([P, P], F32, name="b_rows")
        ident = keep.tile([P, P], F32, name="ident")

        tab32 = tab.bitcast(I32)
        tab_words = {}
        w_planes = {}
        w_words = {}
        u_raw = {}
        placed = {}


        def load_table(first, last):
            tile = keep.tile([P, (last - first) * T], I32, name="tab_words%d" % first, align_bytes=ALIGN)
            rows = tab32[first:last, 0 : P * T].rearrange("a (p t) -> p a t", p=P)
            nc.sync.dma_start(tile[:].rearrange("p (a t) -> p a t", t=T), rows)
            for a in range(first, last):
                tab_words[a] = tile[:, (a - first) * T : (a - first + 1) * T]

        def load_table_scales():
            rows = tab32[:, P * T : P * T + SCALE_ROWS * T].rearrange("a (q r t) -> r q a t", q=4, r=SCALE_ROWS)
            for r in range(SCALE_ROWS):
                queue = nc.sync if r % 2 else nc.scalar
                queue.dma_start(tab_planes[r:P:QUADRANT, :, :], rows[r])

        def clear_w_planes(first, last):
            tile = keep.tile([P, PASSES, (last - first) * P // 4], I32, name="w_planes%d" % first, align_bytes=ALIGN)
            nc.vector.memset(tile[:], 0)
            for m in range(first, last):
                columns = slice((m - first) * P, (m - first + 1) * P)
                w_planes[m] = [tile[:, a, :].bitcast(U8)[:, columns] for a in range(PASSES)]
            return tile

        def load_w_scales(tile, first_tile, first, last):
            rows = w4_scales.bitcast(I32).rearrange("a (q r) n -> r q a n", r=SCALE_ROWS)
            start = first_tile * P // 4
            for r in range(first, last):
                nc.sync.dma_start(tile[r:P:QUADRANT, :, :], rows[r][:, :, start : start + tile.shape[2]])

        def load_u(m):
            tile = keep.tile([P, PACK, P], F32, name="u_raw%d" % m, tag="u_raw%d" % m, align_bytes=ALIGN)
            nc.sync.dma_start(tile[:], u.rearrange("(p i) n -> p i n", i=PACK)[:, :, m * P : (m + 1) * P])
            u_raw[m] = tile[:]

        def load_w(first, last):
            tile = keep.tile([P, PASSES, (last - first) * 2 * P], U8, name="w_words%d" % first, align_bytes=ALIGN)
            rows = w4_words.bitcast(I32).rearrange("a p n -> p a n")
            nc.sync.dma_start(tile[:].bitcast(I32), rows[:, :, first * P // 2 : last * P // 2])
            for m in range(first, last):
                w_words[m] = [tile[:, a, (m - first) * 2 * P : (m - first + 1) * 2 * P] for a in range(PASSES)]

        def clear(m):
            placed[m] = keep.tile([P, T], F32, name="placed%d" % m, align_bytes=ALIGN)
            nc.vector.memset(placed[m][:], 0.0)

        nc.gpsimd.memset(tab_planes[:], 0)
        early_planes = clear_w_planes(0, EARLY_TILES)
        late_planes = {m: clear_w_planes(m, m + 1) for m in range(EARLY_TILES, ROW_TILES)}

        load_table(0, 1)
        nc.sync.dma_start(pick[:], offs)
        load_table_scales()
        nc.sync.dma_start(c_raw[:], c.rearrange("(p i) s -> p i s", i=PACK))
        load_table(1, PASSES)
        load_w_scales(early_planes, 0, 0, 2)
        load_u(0)
        load_w(0, EARLY_TILES)
        load_w_scales(early_planes, 0, 2, SCALE_ROWS)
        load_u(1)
        nc.sync.dma_start(weights[:], wgo)
        nc.sync.dma_start(place[:], offs2)
        load_u(2)
        load_w(EARLY_TILES, ROW_TILES)
        load_w_scales(late_planes[2], 2, 0, SCALE_ROWS)
        load_u(3)
        load_w_scales(late_planes[3], 3, 0, SCALE_ROWS)

        nc.gpsimd.memset(b_rows[:], 0.0)
        nc.gpsimd.dma_start(b_rows[0:ROW_TILES, :], b.rearrange("(m p) -> m p", p=P))
        make_identity(nc, ident[:])
        for m in range(ROW_TILES):
            clear(m)


        def scalar_cast(out_view, in_view):
            nc.scalar.activation(out_view, in_view, COPY)

        def interleave(raw, grouped, cast=scalar_cast):
            cast(grouped[:].rearrange("p (w x) i -> p w i x", x=RUN), raw.rearrange("p i (w x) -> p w i x", x=RUN))
            return grouped

        def grouped_tile(width, name, tag):
            return keep.tile([P, width, PACK], BF16, name=name, tag=tag, align_bytes=ALIGN)

        def quantize(grouped, width, name):
            codes = keep.tile([P, width], U32, name=name + "_codes", tag=name + "_codes", align_bytes=ALIGN)
            scales = keep.tile([P, width], U8, name=name + "_scales", align_bytes=ALIGN)
            nc.vector.quantize_mx(
                out=codes[:].bitcast(FP8X4),
                scales=scales[:],
                in_=grouped[:].rearrange("p w i -> p (w i)"),
            )
            return codes, scales

        got_scales = {}
        got_words = {}
        u_q = {}
        y = {}

        def gather_scales(a):
            got_scales[a] = keep.tile([P, S], U8, name="got_scales%d" % a, align_bytes=ALIGN)
            nc.vector.tensor_copy(got_scales[a][:], tab_planes[:, a, :].bitcast(U8).indirect(pick[:]))

        def gather_words(a, lo, hi, tile=None):
            if tile is None:
                tile = keep.tile([P, hi - lo], U32, name="got_words%d_%d" % (a, lo), align_bytes=ALIGN)
            nc.vector.tensor_copy(tile[:], tab_words[a].bitcast(U32).indirect(pick[:, lo // GROUP : hi // GROUP]))
            got_words[a, lo, hi] = tile[:]
            for x in range(lo, hi, HALF):
                got_words[a, x, x + HALF] = tile[:, x - lo : x - lo + HALF]

        def product(m, lo, hi, bank, order):
            acc = psum.tile([P, hi - lo], F32, name="acc%d_%d" % (m, lo), tag=bank)
            for i, (a, x, end) in enumerate(order):
                if a == DENSE:
                    lhs = u_q[m][0][:].bitcast(FP8X4), u_q[m][1][:]
                    rhs = c_codes[:, x:end], c_scales[:, x:end]
                else:
                    lhs = w_words[m][a].bitcast(FP4X4), w_planes[m][a]
                    rhs = got_words[a, x, end], got_scales[a][:, x:end]
                nc.tensor.matmul_mx(
                    out=acc[:, x - lo : end - lo],
                    lhsT=lhs[0],
                    lhsT_scale=lhs[1],
                    rhs=rhs[0].bitcast(FP8X4),
                    rhs_scale=rhs[1],
                    start=(i == 0),
                    stop=(i == len(order) - 1),
                )
            return acc

        def y_tile(m, tag):
            tile = keep.tile([P, S], F32, name="y%d" % m, tag=tag, align_bytes=ALIGN)
            y[m, 0, S] = tile[:]
            y[m, 0, HALF] = tile[:, 0:HALF]
            y[m, HALF, S] = tile[:, HALF:S]

        def add_bias(acc, m, lo, hi):
            nc.scalar.activation(y[m, lo, hi], acc[:], IDENTITY, bias=bias[:, m : m + 1])

        def scatter(m, lo, hi):
            window = placed[m][:].indirect(place[:, lo // GROUP : hi // GROUP])
            nc.vector.tensor_tensor(window, y[m, lo, hi], weights[:, lo:hi], MULT)

        def store(m):
            nc.sync.dma_start(out[m * P : (m + 1) * P, :], placed[m][:])


        b_t = psum.tile([P, P], F32, name="b_t", tag="bank_b")
        nc.tensor.transpose(b_t[:], b_rows[:], ident[:])
        c_bf = interleave(c_raw[:], grouped_tile(S, "c_bf", "c_bf"))
        u_bf0 = interleave(u_raw[0], grouped_tile(P, "u_bf0", "u_bf0"))
        bias = keep.tile([P, ROW_TILES], F32, name="bias", align_bytes=ALIGN)
        nc.scalar.activation(bias[:], b_t[:, 0:ROW_TILES], COPY)

        gather_words(0, 0, S)
        for a in range(PASSES):
            gather_scales(a)
        gather_words(1, 0, S)
        gather_words(2, 0, HALF)
        c_codes, c_scales = quantize(c_bf, S, "c")
        u_q[0] = quantize(u_bf0, P, "u0")

        acc_first = product(0, 0, HALF, "bank_first", [(a, 0, HALF) for a in (0, 1, 2, DENSE)])

        y_first = keep.tile([P, HALF], F32, name="y_first", align_bytes=ALIGN)
        y[0, 0, HALF] = y_first[:]
        add_bias(acc_first, 0, 0, HALF)
        gather_words(2, HALF, S, keep.tile([P, HALF], U32, name="got_last", tag="u_raw0", align_bytes=ALIGN))
        u_bf1 = interleave(u_raw[1], grouped_tile(P, "u_bf1", "u_bf1"), nc.vector.tensor_copy)
        y_second = keep.tile([P, HALF], F32, name="y_second", align_bytes=ALIGN)
        y[0, HALF, S] = y_second[:]
        acc_second = product(0, HALF, S, "bank_even", [(a, HALF, S) for a in (0, 1, DENSE, 2)])
        add_bias(acc_second, 0, HALF, S)

        scatter(0, 0, HALF)
        u_q[1] = quantize(u_bf1, P, "u1")
        u_bf2 = interleave(u_raw[2], grouped_tile(P, "u_bf2", "u_bf2"))
        whole = [(2, HALF, S), (2, 0, HALF), (0, 0, S), (1, 0, S), (DENSE, 0, S)]
        acc1 = product(1, 0, S, "bank_odd", whole)
        y_tile(1, "u_raw2")
        add_bias(acc1, 1, 0, S)
        scatter(0, HALF, S)
        store(0)

        u_q[2] = quantize(u_bf2, P, "u2")
        u_bf3 = interleave(u_raw[3], grouped_tile(P, "u_bf3", "u0_codes"))
        scatter(1, 0, S)
        store(1)

        u_q[3] = quantize(u_bf3, P, "u3")
        acc2 = product(2, 0, S, "bank_even", whole)
        y_tile(2, "u_raw3")
        add_bias(acc2, 2, 0, S)
        acc3 = product(3, 0, S, "bank_odd", whole)
        y_tile(3, "y3")
        add_bias(acc3, 3, 0, S)
        scatter(2, 0, S)
        store(2)
        scatter(3, 0, S)
        store(3)
